import numpy as np
import ml_dtypes


def mxq(x, axis, fmt="e4m3"):
    dtype, down = {"e4m3": (ml_dtypes.float8_e4m3fn, 7), "e5m2": (ml_dtypes.float8_e5m2, 14)}[fmt]
    v = np.moveaxis(np.asarray(x, np.float32).astype(ml_dtypes.bfloat16).astype(np.float64), axis, -1)
    blocks = v.reshape(v.shape[:-1] + (-1, 32))
    amax = np.abs(blocks).max(-1, keepdims=True)
    byte = np.maximum(np.where(amax > 0, np.frexp(amax)[1] - 1 + 127, 0) - down, 1)
    scale = np.exp2(byte - 127.0)
    codes = (blocks / scale).astype(np.float32).astype(dtype).astype(np.float64)
    return np.moveaxis((codes * scale).reshape(v.shape), -1, axis)


WIDE = False


def mx_kscale(k):
    if not WIDE:
        return np.ones(k)
    levels = np.array([24, -24, 12, -12, 0])
    if k % 512:
        return np.exp2(np.random.permutation(np.resize(levels, k // 32))).repeat(32)
    a = np.empty((k // 512, 16))
    for p in range(k // 512):
        a[p, :8] = np.random.permutation(np.resize(levels, 8))
        for g in range(8):
            far = levels[np.abs(levels - a[p, g]) >= 10]
            a[p, g + 8] = far[np.random.randint(len(far))]
    return np.exp2(a.ravel()).repeat(32)


def f64(x):
    return np.asarray(x).astype(np.float64)


def striped(idx):
    return np.tile(idx.reshape(-1, 16).T, (8, 1)).astype(np.uint16)


def unstriped(offs):
    return offs[:16].T.reshape(-1).astype(np.int64)


E2M1 = np.array([0.0, 0.5, 1.0, 1.5, 2.0, 3.0, 4.0, 6.0, -0.0, -0.5, -1.0, -1.5, -2.0, -3.0, -4.0, -6.0])


def pack_weight(w, fmt):
    k, n = w.shape
    w = f64(np.asarray(w, np.float32).astype(ml_dtypes.bfloat16)).reshape(k // 32, 32, n)
    amax = np.abs(w).max(1)
    if fmt == "e4m3":
        byte = np.frexp(amax)[1] - 1 + 127 - 7
    else:
        mant, ex = np.frexp(amax / 6.0)
        byte = np.where(mant > 0.5, ex, ex - 1) + 127
    byte = np.clip(np.where(amax > 0, byte, 1), 1, 254)
    scaled = (w * np.exp2(127.0 - byte)[:, None, :]).reshape(k, n).astype(np.float32)
    by_word = np.ascontiguousarray(scaled.reshape(k // 512, 128, 4, n).transpose(0, 1, 3, 2))
    if fmt == "e4m3":
        words = by_word.astype(ml_dtypes.float8_e4m3fn).view(np.uint8)
    else:
        c = by_word.astype(ml_dtypes.float4_e2m1fn).view(np.uint8) & 0xF
        words = (c[..., 0::2] | (c[..., 1::2] << 4)).reshape(k // 512, 128, 2 * n)
    return np.ascontiguousarray(words), np.ascontiguousarray(byte.astype(np.uint8).reshape(k // 512, 16, n))


def unpack_weight(words, scales, fmt):
    g, _, n = scales.shape
    words = np.ascontiguousarray(words).reshape(g, 128, n, -1)
    if fmt == "e4m3":
        vals = words.view(ml_dtypes.float8_e4m3fn).astype(np.float64)
    else:
        nib = np.empty((g, 128, n, 4), np.uint8)
        nib[..., 0::2] = words & 0xF
        nib[..., 1::2] = words >> 4
        vals = E2M1[nib]
    vals = vals * np.repeat(np.exp2(scales.astype(np.float64) - 127.0), 8, axis=1)[..., None]
    return vals.transpose(0, 1, 3, 2).reshape(g * 512, n)


def pack_table4(v):
    words, scales = pack_weight(v, "e2m1")
    g, t = words.shape[0] // 2, v.shape[1]
    return np.ascontiguousarray(words.reshape(g, 2, 128, t, 2).transpose(0, 2, 3, 1, 4).reshape(g, 128, t, 4)), scales


def unpack_table4(words, scales):
    g, _, t, _ = words.shape
    return unpack_weight(words.reshape(g, 128, t, 2, 2).transpose(0, 3, 1, 2, 4).reshape(2 * g, 128, 2 * t), scales, "e2m1")


def silu(f):
    return f / (1.0 + np.exp(-np.maximum(f, -700.0)))


K, L, N, T, J = 1024, 512, 512, 4096, 512


def setup_inputs():
    n = np.random.standard_normal
    s = mx_kscale(K)[:, None]
    s2 = mx_kscale(L)[:, None]
    p_tab = pack_table4(n((K, T)) * s)
    p_w = pack_weight(n((K, N)) / np.sqrt(K) / s, "e2m1")
    p_wx = pack_weight(n((L, N)) / np.sqrt(L) / s2, "e2m1")
    return {
        "tab_words": p_tab[0],
        "tab_scales": p_tab[1],
        "w_words": p_w[0],
        "w_scales": p_w[1],
        "x": (n((L, J)) * s2).astype(np.float32),
        "wx_words": p_wx[0],
        "wx_scales": p_wx[1],
        "iw0": (np.random.uniform(0.1, 0.6, J)).astype(np.float32),
        "iw1": (np.random.uniform(0.1, 0.6, J)).astype(np.float32),
        "iw2": (np.random.uniform(0.1, 0.6, J)).astype(np.float32),
        "iw3": (np.random.uniform(0.1, 0.6, J)).astype(np.float32),
        "b": (0.3 * n(N)).astype(np.float32),
        "offs": striped(np.concatenate([np.random.permutation(T)[:J] for _ in range(4)])),
    }


def reference(tab_words, tab_scales, w_words, w_scales, x, wx_words, wx_scales, iw0, iw1, iw2, iw3, b, offs):
    idx = unstriped(offs).reshape(4, J)
    tab_ = unpack_table4(tab_words, tab_scales)[:, idx]
    w_ = unpack_weight(w_words, w_scales, "e2m1")
    a0 = w_.T @ tab_[:, 0]
    a1 = w_.T @ tab_[:, 1]
    a2 = w_.T @ tab_[:, 2]
    a3 = w_.T @ tab_[:, 3]
    x_ = mxq(f64(x), 0, "e4m3")
    wx_ = unpack_weight(wx_words, wx_scales, "e2m1")
    ax = wx_.T @ x_
    return silu(a0 * f64(iw0)[None, :] + a1 * f64(iw1)[None, :] + a2 * f64(iw2)[None, :] + a3 * f64(iw3)[None, :] + ax + f64(b)[:, None])

@@ -1,0 +1,200 @@
+from contextlib import ExitStack
+
+import concourse.mybir as mybir
+
+K, L, N, T, J = 1024, 512, 512, 4096, 512
+G = 4
+P = 128
+FLOPS = 2 * N * J * (G * K + L)
+
+F32 = mybir.dt.float32
+BF16 = mybir.dt.bfloat16
+I32 = mybir.dt.int32
+U32 = mybir.dt.uint32
+U16 = mybir.dt.uint16
+U8 = mybir.dt.uint8
+FP8X4 = mybir.dt.float8_e4m3fn_x4
+FP4X4 = mybir.dt.float4_e2m1fn_x4
+ACT = mybir.ActivationFunctionType
+ALU = mybir.AluOpType
+
+JT = J // P
+NT = N // P
+LIST_COLS = J // 16
+
+
+def tile_list_interp_silu_kernel(
+    tc, tab_words, tab_scales, w_words, w_scales, x, wx_words, wx_scales, iw0, iw1, iw2, iw3, b, offs, out
+):
+    nc = tc.nc
+    with ExitStack() as ctx:
+        held = ctx.enter_context(tc.tile_pool(name="held", bufs=1))
+        acc_pool = ctx.enter_context(tc.psum_pool(name="acc", bufs=4))
+        fin_pool = ctx.enter_context(tc.psum_pool(name="fin", bufs=1))
+
+        def sb(name, shape, dtype, tag=None):
+            return held.tile(shape, dtype, name=name, tag=tag or name, align_bytes=64)
+
+        offsets = held.tile([P, G * LIST_COLS], U16, name="offsets")
+        nc.sync.dma_start(offsets[:], offs)
+
+        x_raw = sb("x_raw", [P, 4, J], F32, tag="x_then_w")
+        nc.sync.dma_start(x_raw[:], x.rearrange("(p i) j -> p i j", i=4))
+        wx_sb = sb("wx_sb", [P, 2 * N], U8)
+        nc.sync.dma_start(wx_sb[:].bitcast(I32), wx_words[0].bitcast(I32))
+        b_stage = sb("b_stage", [P, P], F32)
+        nc.gpsimd.memset(b_stage[:], 0.0)
+        nc.sync.dma_start(b_stage[0:NT, :], b.rearrange("(t p) -> t p", p=P))
+
+        scale_table = sb("scale_table", [P, T // 4], I32)
+        nc.vector.memset(scale_table[:], 0)
+        scale_rows = tab_scales.bitcast(I32).rearrange("a (q r) t -> r q a t", r=4)
+        for r in range(4):
+            nc.sync.dma_start(scale_table[r:P:16, :], scale_rows[r])
+
+        zeros = sb("zeros", [P, P], F32, tag="zeros_then_table")
+        nc.vector.memset(zeros[:], 0.0)
+        warm = sb("warm", [P, 16], F32)
+        nc.vector.memset(warm[:, 0:1], 0.0)
+        nc.scalar.activation(warm[:, 8:9], warm[:, 0:1], ACT.Silu)
+
+        ident = sb("ident", [P, P], F32)
+        nc.gpsimd.affine_select(
+            out=ident[:], in_=zeros[:], compare_op=ALU.not_equal, fill=1.0, base=0, pattern=[[-1, P]], channel_multiplier=1
+        )
+        stage_bank = acc_pool.tile([P, P], F32, name="bank")
+        nc.tensor.transpose(stage_bank[:], b_stage[:], ident[:])
+        b_cols = sb("b_cols", [P, NT], F32)
+        nc.vector.tensor_copy(b_cols[:], stage_bank[:, 0:NT])
+
+        word_table = sb("word_table", [P, T], I32, tag="zeros_then_table")
+        nc.sync.dma_start(word_table[:], tab_words[0].rearrange("p t c -> p (t c)").bitcast(I32))
+
+        wx_plane = sb("wx_plane", [P, N // 4], I32)
+        w_planes = sb("w_planes", [P, 2, N // 4], I32)
+        picked_scales = [sb(f"picked_scales{h}", [P, 2 * J], U8) for h in range(2)]
+        shifted_scales = [sb(f"shifted_scales{h}", [P, 2 * J // 4], I32) for h in range(2)]
+        nc.gpsimd.memset(wx_plane[:], 0)
+        for q in range(4):
+            nc.gpsimd.dma_start(wx_plane[32 * q : 32 * q + 4, :], wx_scales.bitcast(I32)[0, 4 * q : 4 * q + 4, :])
+            if q == 1:
+                nc.gpsimd.memset(w_planes[:], 0)
+                for h in range(2):
+                    nc.gpsimd.memset(shifted_scales[h][96:P, :], 0)
+        for q in range(4):
+            nc.sync.dma_start(
+                w_planes[32 * q : 32 * q + 4, :, :],
+                w_scales.bitcast(I32)[:, 4 * q : 4 * q + 4, :].rearrange("a r n -> r a n"),
+            )
+        iw_cols = []
+        for g, iw in enumerate((iw0, iw1, iw2, iw3)):
+            cols = sb(f"iw_cols{g}", [P, JT], F32)
+            with nc.allow_non_contiguous_dma(reason="one weight a partition"):
+                nc.gpsimd.dma_start(cols[:], iw.rearrange("(t p) -> p t", p=P))
+            iw_cols.append(cols)
+
+        final = [fin_pool.tile([P, NT, P], F32, name=f"final{jt}") for jt in range(JT)]
+
+        def add_transposed(jt, part, first, last):
+            for nt in range(NT):
+                nc.tensor.matmul(
+                    final[jt][:, nt, :],
+                    lhsT=part[:, nt * P : (nt + 1) * P],
+                    rhs=ident[:],
+                    is_transpose=True,
+                    start=(first and nt == 0),
+                    stop=(last and nt == NT - 1),
+                )
+
+        b_bank = acc_pool.tile([P, N], F32, name="bank")
+        for nt in range(NT):
+            nc.tensor.transpose(b_bank[:, nt * P : (nt + 1) * P], b_cols[:, nt : nt + 1].to_broadcast([P, P]), ident[:])
+        b_rows = sb("b_rows", [P, N], F32)
+        nc.scalar.copy(b_rows[:], b_bank[:])
+        for jt in range(JT):
+            add_transposed(jt, b_rows, True, False)
+
+        x_codes = sb("x_codes", [P, J], U32)
+        x_plane = sb("x_plane", [P, J], U8)
+        for h in range(2):
+            cols = slice(h * J // 2, (h + 1) * J // 2)
+            x_bf = sb(f"x_bf{h}", [P, J // 2, 4], BF16)
+            nc.scalar.copy(x_bf[:], x_raw[:, :, cols].rearrange("p i j -> p j i"))
+            nc.vector.quantize_mx(
+                out=x_codes[:, cols].bitcast(FP8X4), scales=x_plane[:, cols], in_=x_bf[:].rearrange("p j i -> p (j i)")
+            )
+        w_sb = sb("w_sb", [P, 2, 2 * N], U8, tag="x_then_w")
+        nc.sync.dma_start(w_sb[:].bitcast(I32), w_words.bitcast(I32).rearrange("a p n -> p a n"))
+        for jt in range(JT):
+            cols = slice(jt * P, (jt + 1) * P)
+            bank = acc_pool.tile([P, N], F32, name="bank")
+            nc.tensor.matmul_mx(
+                out=bank[:],
+                lhsT=x_codes[:, cols].bitcast(FP8X4),
+                lhsT_scale=x_plane[:, cols],
+                rhs=wx_sb[:].bitcast(FP4X4),
+                rhs_scale=wx_plane[:].bitcast(U8),
+                start=True,
+                stop=True,
+            )
+            skip = sb(f"skip{jt}", [P, N], F32)
+            nc.scalar.copy(skip[:], bank[:])
+            add_transposed(jt, skip, False, False)
+
+        for g in range(G):
+            h, u = divmod(g, 2)
+            nc.vector.tensor_copy(
+                picked_scales[h][:, u * J : (u + 1) * J],
+                scale_table[:].bitcast(U8).indirect(offsets[:, g * LIST_COLS : (g + 1) * LIST_COLS]),
+            )
+            if u == 1:
+                nc.scalar.dma_start(shifted_scales[h][0 : P - 16, :], picked_scales[h][16:P, :].bitcast(I32))
+
+        parted = []
+        for g in range(G):
+            picked = sb(f"picked{g}", [P, J], U32)
+            nc.vector.tensor_copy(
+                picked[:], word_table[:].bitcast(U32).indirect(offsets[:, g * LIST_COLS : (g + 1) * LIST_COLS])
+            )
+            halves = sb(f"parted{g}", [P, 2, 2 * J], U8)
+            nc.vector.tensor_copy(halves[:].bitcast(U16), picked[:].bitcast(U16).rearrange("p (j d) -> p d j", d=2))
+            parted.append(halves)
+
+        def project(g, jt):
+            h, u = divmod(g, 2)
+            bank = acc_pool.tile([P, N], F32, name="bank")
+            c0 = u * J + jt * P
+            planes = (picked_scales[h][:], shifted_scales[h][:].bitcast(U8))
+            for a in range(2):
+                nc.tensor.matmul_mx(
+                    out=bank[:],
+                    lhsT=parted[g][:, a, 2 * jt * P : 2 * (jt + 1) * P].bitcast(FP4X4),
+                    lhsT_scale=planes[a][:, c0 : c0 + P],
+                    rhs=w_sb[:, a, :].bitcast(FP4X4),
+                    rhs_scale=w_planes[:, a, :].bitcast(U8),
+                    start=(a == 0),
+                    stop=(a == 1),
+                )
+            return bank
+
+        parts = {}
+        for g in range(G):
+            for jt in range(JT):
+                bank = project(g, jt)
+                part = sb(f"part{g}_{jt}", [P, N], F32)
+                weight = iw_cols[g][:, jt : jt + 1]
+                if g < 2:
+                    nc.scalar.activation(part[:], bank[:], ACT.Copy, scale=weight)
+                else:
+                    nc.vector.scalar_tensor_tensor(part[:], bank[:], weight, parts[g - 1, jt][:], ALU.mult, ALU.add)
+                parts[g, jt] = part
+            if g == 2:
+                for jt in range(JT):
+                    add_transposed(jt, parts[0, jt], False, False)
+
+        out_view = out.rearrange("(t p) j -> p t j", p=P)
+        for jt in range(JT):
+            add_transposed(jt, parts[G - 1, jt], False, True)
+            result = sb(f"result{jt}", [P, NT, P], F32)
+            nc.scalar.activation(result[:], final[jt][:], ACT.Silu)
+            nc.sync.dma_start(out_view[:, :, jt * P : (jt + 1) * P], result[:])

@@ -1,6 +1,7 @@
 from contextlib import ExitStack
 
 import concourse.mybir as mybir
+from concourse.masks import make_identity
 
 K, L, N, T, J = 1024, 512, 512, 4096, 512
 G = 4
@@ -21,6 +22,7 @@ ALU = mybir.AluOpType
 JT = J // P
 NT = N // P
 LIST_COLS = J // 16
+ZERO_SPLIT = 512
 
 
 def tile_list_interp_silu_kernel(
@@ -38,60 +40,45 @@ def tile_list_interp_silu_kernel(
         offsets = held.tile([P, G * LIST_COLS], U16, name="offsets")
         nc.sync.dma_start(offsets[:], offs)
 
-        x_raw = sb("x_raw", [P, 4, J], F32, tag="x_then_w")
-        nc.sync.dma_start(x_raw[:], x.rearrange("(p i) j -> p i j", i=4))
-        wx_sb = sb("wx_sb", [P, 2 * N], U8)
-        nc.sync.dma_start(wx_sb[:].bitcast(I32), wx_words[0].bitcast(I32))
-        b_stage = sb("b_stage", [P, P], F32)
-        nc.gpsimd.memset(b_stage[:], 0.0)
-        nc.sync.dma_start(b_stage[0:NT, :], b.rearrange("(t p) -> t p", p=P))
-
+        wx_plane = sb("wx_plane", [P, N // 4], I32)
+        nc.gpsimd.memset(wx_plane[:], 0)
         scale_table = sb("scale_table", [P, T // 4], I32)
-        nc.vector.memset(scale_table[:], 0)
+        nc.gpsimd.memset(scale_table[:, 0:ZERO_SPLIT], 0)
+        nc.vector.memset(scale_table[:, ZERO_SPLIT:], 0)
         scale_rows = tab_scales.bitcast(I32).rearrange("a (q r) t -> r q a t", r=4)
         for r in range(4):
             nc.sync.dma_start(scale_table[r:P:16, :], scale_rows[r])
+        wx_sb = sb("wx_sb", [P, 2 * N], U8)
+        nc.sync.dma_start(wx_sb[:].bitcast(I32), wx_words[0].bitcast(I32))
+        x_raw = sb("x_raw", [P, 4, J], F32)
+        for q in range(4):
+            if q == 1:
+                nc.sync.dma_start(x_raw[:], x.rearrange("(p i) j -> p i j", i=4))
+            nc.sync.dma_start(wx_plane[32 * q : 32 * q + 4, :], wx_scales.bitcast(I32)[0, 4 * q : 4 * q + 4, :])
+        word_table = sb("word_table", [P, T], I32)
+        nc.sync.dma_start(word_table[:], tab_words[0].rearrange("p t c -> p (t c)").bitcast(I32))
 
-        zeros = sb("zeros", [P, P], F32, tag="zeros_then_table")
-        nc.vector.memset(zeros[:], 0.0)
         warm = sb("warm", [P, 16], F32)
         nc.vector.memset(warm[:, 0:1], 0.0)
         nc.scalar.activation(warm[:, 8:9], warm[:, 0:1], ACT.Silu)
 
-        ident = sb("ident", [P, P], F32)
-        nc.gpsimd.affine_select(
-            out=ident[:], in_=zeros[:], compare_op=ALU.not_equal, fill=1.0, base=0, pattern=[[-1, P]], channel_multiplier=1
-        )
-        stage_bank = acc_pool.tile([P, P], F32, name="bank")
-        nc.tensor.transpose(stage_bank[:], b_stage[:], ident[:])
-        b_cols = sb("b_cols", [P, NT], F32)
-        nc.vector.tensor_copy(b_cols[:], stage_bank[:, 0:NT])
-
-        word_table = sb("word_table", [P, T], I32, tag="zeros_then_table")
-        nc.sync.dma_start(word_table[:], tab_words[0].rearrange("p t c -> p (t c)").bitcast(I32))
-
-        wx_plane = sb("wx_plane", [P, N // 4], I32)
+        w_sb = sb("w_sb", [P, 2, 2 * N], U8)
+        nc.sync.dma_start(w_sb[:].bitcast(I32), w_words.bitcast(I32).rearrange("a p n -> p a n"))
         w_planes = sb("w_planes", [P, 2, N // 4], I32)
-        picked_scales = [sb(f"picked_scales{h}", [P, 2 * J], U8) for h in range(2)]
-        shifted_scales = [sb(f"shifted_scales{h}", [P, 2 * J // 4], I32) for h in range(2)]
-        nc.gpsimd.memset(wx_plane[:], 0)
-        for q in range(4):
-            nc.gpsimd.dma_start(wx_plane[32 * q : 32 * q + 4, :], wx_scales.bitcast(I32)[0, 4 * q : 4 * q + 4, :])
-            if q == 1:
-                nc.gpsimd.memset(w_planes[:], 0)
-                for h in range(2):
-                    nc.gpsimd.memset(shifted_scales[h][96:P, :], 0)
+        nc.vector.memset(w_planes[:], 0)
         for q in range(4):
             nc.sync.dma_start(
                 w_planes[32 * q : 32 * q + 4, :, :],
                 w_scales.bitcast(I32)[:, 4 * q : 4 * q + 4, :].rearrange("a r n -> r a n"),
             )
-        iw_cols = []
-        for g, iw in enumerate((iw0, iw1, iw2, iw3)):
-            cols = sb(f"iw_cols{g}", [P, JT], F32)
-            with nc.allow_non_contiguous_dma(reason="one weight a partition"):
-                nc.gpsimd.dma_start(cols[:], iw.rearrange("(t p) -> p t", p=P))
-            iw_cols.append(cols)
+
+        picked_scales = [sb(f"picked_scales{h}", [P, 2 * J], U8) for h in range(2)]
+        shifted_scales = [sb(f"shifted_scales{h}", [P, 2 * J // 4], I32) for h in range(2)]
+        for h in range(2):
+            nc.vector.memset(shifted_scales[h][96:P, :], 0)
+        ident = sb("ident", [P, P], F32)
+        nc.vector.memset(ident[:], 0.0)
+        make_identity(nc, ident[:], nomemset=True)
 
         final = [fin_pool.tile([P, NT, P], F32, name=f"final{jt}") for jt in range(JT)]
 
@@ -106,25 +93,15 @@ def tile_list_interp_silu_kernel(
                     stop=(last and nt == NT - 1),
                 )
 
-        b_bank = acc_pool.tile([P, N], F32, name="bank")
-        for nt in range(NT):
-            nc.tensor.transpose(b_bank[:, nt * P : (nt + 1) * P], b_cols[:, nt : nt + 1].to_broadcast([P, P]), ident[:])
-        b_rows = sb("b_rows", [P, N], F32)
-        nc.scalar.copy(b_rows[:], b_bank[:])
-        for jt in range(JT):
-            add_transposed(jt, b_rows, True, False)
-
         x_codes = sb("x_codes", [P, J], U32)
         x_plane = sb("x_plane", [P, J], U8)
         for h in range(2):
             cols = slice(h * J // 2, (h + 1) * J // 2)
-            x_bf = sb(f"x_bf{h}", [P, J // 2, 4], BF16)
+            x_bf = sb(f"x_bf{h}", [P, J // 2, 4], BF16, tag=f"x_bf{h}")
             nc.scalar.copy(x_bf[:], x_raw[:, :, cols].rearrange("p i j -> p j i"))
             nc.vector.quantize_mx(
                 out=x_codes[:, cols].bitcast(FP8X4), scales=x_plane[:, cols], in_=x_bf[:].rearrange("p j i -> p (j i)")
             )
-        w_sb = sb("w_sb", [P, 2, 2 * N], U8, tag="x_then_w")
-        nc.sync.dma_start(w_sb[:].bitcast(I32), w_words.bitcast(I32).rearrange("a p n -> p a n"))
         for jt in range(JT):
             cols = slice(jt * P, (jt + 1) * P)
             bank = acc_pool.tile([P, N], F32, name="bank")
@@ -139,7 +116,13 @@ def tile_list_interp_silu_kernel(
             )
             skip = sb(f"skip{jt}", [P, N], F32)
             nc.scalar.copy(skip[:], bank[:])
-            add_transposed(jt, skip, False, False)
+            add_transposed(jt, skip, True, False)
+
+        columns = sb("columns", [P, G + 1, 8], F32)
+
+        def load_column(slot, vec):
+            with nc.allow_non_contiguous_dma(reason="one value a partition"):
+                nc.sync.dma_start(columns[:, slot, 0:JT], vec.rearrange("(t p) -> p t", p=P))
 
         for g in range(G):
             h, u = divmod(g, 2)
@@ -148,7 +131,11 @@ def tile_list_interp_silu_kernel(
                 scale_table[:].bitcast(U8).indirect(offsets[:, g * LIST_COLS : (g + 1) * LIST_COLS]),
             )
             if u == 1:
-                nc.scalar.dma_start(shifted_scales[h][0 : P - 16, :], picked_scales[h][16:P, :].bitcast(I32))
+                nc.sync.dma_start(shifted_scales[h][0 : P - 16, :], picked_scales[h][16:P, :].bitcast(I32))
+                if h == 0:
+                    load_column(0, iw0)
+        for slot, vec in ((1, iw1), (2, iw2), (3, iw3), (4, b)):
+            load_column(slot, vec)
 
         parted = []
         for g in range(G):
@@ -157,7 +144,11 @@ def tile_list_interp_silu_kernel(
                 picked[:], word_table[:].bitcast(U32).indirect(offsets[:, g * LIST_COLS : (g + 1) * LIST_COLS])
             )
             halves = sb(f"parted{g}", [P, 2, 2 * J], U8)
-            nc.vector.tensor_copy(halves[:].bitcast(U16), picked[:].bitcast(U16).rearrange("p (j d) -> p d j", d=2))
+            pieces = (0, P, J) if g == 0 else (0, J)
+            for c0, c1 in zip(pieces, pieces[1:]):
+                nc.vector.tensor_copy(
+                    halves[:].bitcast(U16)[:, :, c0:c1], picked[:, c0:c1].bitcast(U16).rearrange("p (j d) -> p d j", d=2)
+                )
             parted.append(halves)
 
         def project(g, jt):
@@ -182,19 +173,19 @@ def tile_list_interp_silu_kernel(
             for jt in range(JT):
                 bank = project(g, jt)
                 part = sb(f"part{g}_{jt}", [P, N], F32)
-                weight = iw_cols[g][:, jt : jt + 1]
+                weight = columns[:, g, jt : jt + 1]
                 if g < 2:
                     nc.scalar.activation(part[:], bank[:], ACT.Copy, scale=weight)
                 else:
                     nc.vector.scalar_tensor_tensor(part[:], bank[:], weight, parts[g - 1, jt][:], ALU.mult, ALU.add)
                 parts[g, jt] = part
-            if g == 2:
-                for jt in range(JT):
-                    add_transposed(jt, parts[0, jt], False, False)
 
         out_view = out.rearrange("(t p) j -> p t j", p=P)
         for jt in range(JT):
+            add_transposed(jt, parts[0, jt], False, False)
             add_transposed(jt, parts[G - 1, jt], False, True)
             result = sb(f"result{jt}", [P, NT, P], F32)
-            nc.scalar.activation(result[:], final[jt][:], ACT.Silu)
-            nc.sync.dma_start(out_view[:, :, jt * P : (jt + 1) * P], result[:])
+            for nt in range(NT):
+                nc.scalar.activation(result[:, nt, :], final[jt][:, nt, :], ACT.Silu, bias=columns[:, G, nt : nt + 1])
+                if nt % 2 == 1:
+                    nc.sync.dma_start(out_view[:, nt - 1 : nt + 1, jt * P : (jt + 1) * P], result[:, nt - 1 : nt + 1, :])

@@ -22,7 +22,6 @@ ALU = mybir.AluOpType
 JT = J // P
 NT = N // P
 LIST_COLS = J // 16
-ZERO_SPLIT = 512
 
 
 def tile_list_interp_silu_kernel(
@@ -41,20 +40,22 @@ def tile_list_interp_silu_kernel(
         nc.sync.dma_start(offsets[:], offs)
 
         wx_plane = sb("wx_plane", [P, N // 4], I32)
-        nc.gpsimd.memset(wx_plane[:], 0)
+        nc.vector.memset(wx_plane[:], 0)
         scale_table = sb("scale_table", [P, T // 4], I32)
-        nc.gpsimd.memset(scale_table[:, 0:ZERO_SPLIT], 0)
-        nc.vector.memset(scale_table[:, ZERO_SPLIT:], 0)
+        nc.gpsimd.memset(scale_table[:, 0 : T // 8], 0)
+        nc.vector.memset(scale_table[:, T // 8 :], 0)
         scale_rows = tab_scales.bitcast(I32).rearrange("a (q r) t -> r q a t", r=4)
         for r in range(4):
             nc.sync.dma_start(scale_table[r:P:16, :], scale_rows[r])
         wx_sb = sb("wx_sb", [P, 2 * N], U8)
         nc.sync.dma_start(wx_sb[:].bitcast(I32), wx_words[0].bitcast(I32))
-        x_raw = sb("x_raw", [P, 4, J], F32)
+        x_rows = x.rearrange("(p i) j -> p i j", i=4)
+        x_raw = [sb(f"x_raw{h}", [P, 4, J // 2], F32) for h in range(2)]
         for q in range(4):
-            if q == 1:
-                nc.sync.dma_start(x_raw[:], x.rearrange("(p i) j -> p i j", i=4))
             nc.sync.dma_start(wx_plane[32 * q : 32 * q + 4, :], wx_scales.bitcast(I32)[0, 4 * q : 4 * q + 4, :])
+            if q == 0:
+                for h in range(2):
+                    nc.sync.dma_start(x_raw[h][:], x_rows[:, :, h * J // 2 : (h + 1) * J // 2])
         word_table = sb("word_table", [P, T], I32)
         nc.sync.dma_start(word_table[:], tab_words[0].rearrange("p t c -> p (t c)").bitcast(I32))
 
@@ -72,7 +73,6 @@ def tile_list_interp_silu_kernel(
                 w_scales.bitcast(I32)[:, 4 * q : 4 * q + 4, :].rearrange("a r n -> r a n"),
             )
 
-        picked_scales = [sb(f"picked_scales{h}", [P, 2 * J], U8) for h in range(2)]
         shifted_scales = [sb(f"shifted_scales{h}", [P, 2 * J // 4], I32) for h in range(2)]
         for h in range(2):
             nc.vector.memset(shifted_scales[h][96:P, :], 0)
@@ -95,10 +95,11 @@ def tile_list_interp_silu_kernel(
 
         x_codes = sb("x_codes", [P, J], U32)
         x_plane = sb("x_plane", [P, J], U8)
-        for h in range(2):
-            cols = slice(h * J // 2, (h + 1) * J // 2)
-            x_bf = sb(f"x_bf{h}", [P, J // 2, 4], BF16, tag=f"x_bf{h}")
-            nc.scalar.copy(x_bf[:], x_raw[:, :, cols].rearrange("p i j -> p j i"))
+        for jt in range(JT):
+            cols = slice(jt * P, (jt + 1) * P)
+            h, u = divmod(jt, 2)
+            x_bf = sb(f"x_bf{jt}", [P, P, 4], BF16)
+            nc.scalar.copy(x_bf[:], x_raw[h][:, :, u * P : (u + 1) * P].rearrange("p i j -> p j i"))
             nc.vector.quantize_mx(
                 out=x_codes[:, cols].bitcast(FP8X4), scales=x_plane[:, cols], in_=x_bf[:].rearrange("p j i -> p (j i)")
             )
@@ -119,6 +120,7 @@ def tile_list_interp_silu_kernel(
             add_transposed(jt, skip, True, False)
 
         columns = sb("columns", [P, G + 1, 8], F32)
+        picked_scales = [sb("picked_scales0", [P, 2 * J], U8), sb("picked_scales1", [P, 2 * J], U8, tag="x_bf1")]
 
         def load_column(slot, vec):
             with nc.allow_non_contiguous_dma(reason="one value a partition"):
@@ -136,6 +138,18 @@ def tile_list_interp_silu_kernel(
                     load_column(0, iw0)
         for slot, vec in ((1, iw1), (2, iw2), (3, iw3), (4, b)):
             load_column(slot, vec)
+
+        warm_bank = acc_pool.tile([P, N], F32, name="bank")
+        for i in range(3):
+            nc.tensor.matmul_mx(
+                out=warm_bank[:],
+                lhsT=wx_sb[:, 0 : 2 * P].bitcast(FP4X4),
+                lhsT_scale=picked_scales[1][:, J : J + P],
+                rhs=wx_sb[:].bitcast(FP4X4),
+                rhs_scale=wx_plane[:].bitcast(U8),
+                start=(i == 0),
+                stop=(i == 2),
+            )
 
         parted = []
         for g in range(G):

@@ -140,7 +140,7 @@ def tile_list_interp_silu_kernel(
             load_column(slot, vec)
 
         warm_bank = acc_pool.tile([P, N], F32, name="bank")
-        for i in range(3):
+        for i in range(2):
             nc.tensor.matmul_mx(
                 out=warm_bank[:],
                 lhsT=wx_sb[:, 0 : 2 * P].bitcast(FP4X4),
@@ -148,7 +148,7 @@ def tile_list_interp_silu_kernel(
                 rhs=wx_sb[:].bitcast(FP4X4),
                 rhs_scale=wx_plane[:].bitcast(U8),
                 start=(i == 0),
-                stop=(i == 2),
+                stop=(i == 1),
             )
 
         parted = []
@@ -158,7 +158,7 @@ def tile_list_interp_silu_kernel(
                 picked[:], word_table[:].bitcast(U32).indirect(offsets[:, g * LIST_COLS : (g + 1) * LIST_COLS])
             )
             halves = sb(f"parted{g}", [P, 2, 2 * J], U8)
-            pieces = (0, P, J) if g == 0 else (0, J)
+            pieces = (0, P, J) if g < 2 else (0, J)
             for c0, c1 in zip(pieces, pieces[1:]):
                 nc.vector.tensor_copy(
                     halves[:].bitcast(U16)[:, :, c0:c1], picked[:, c0:c1].bitcast(U16).rearrange("p (j d) -> p d j", d=2)

@@ -30,7 +30,7 @@ def tile_list_interp_silu_kernel(
     nc = tc.nc
     with ExitStack() as ctx:
         held = ctx.enter_context(tc.tile_pool(name="held", bufs=1))
-        acc_pool = ctx.enter_context(tc.psum_pool(name="acc", bufs=4))
+        acc_pool = ctx.enter_context(tc.psum_pool(name="acc", bufs=1))
         fin_pool = ctx.enter_context(tc.psum_pool(name="fin", bufs=1))
 
         def sb(name, shape, dtype, tag=None):
@@ -39,46 +39,59 @@ def tile_list_interp_silu_kernel(
         offsets = held.tile([P, G * LIST_COLS], U16, name="offsets")
         nc.sync.dma_start(offsets[:], offs)
 
+        scale_table = sb("scale_table", [P, T // 4], I32)
+        nc.sync.dma_start(scale_table[96:P, :], tab_scales.bitcast(I32).rearrange("a q t -> (a q) t"))
         wx_plane = sb("wx_plane", [P, N // 4], I32)
         nc.vector.memset(wx_plane[:], 0)
-        scale_table = sb("scale_table", [P, T // 4], I32)
-        nc.gpsimd.memset(scale_table[:, 0 : T // 8], 0)
-        nc.vector.memset(scale_table[:, T // 8 :], 0)
-        scale_rows = tab_scales.bitcast(I32).rearrange("a (q r) t -> r q a t", r=4)
-        for r in range(4):
-            nc.sync.dma_start(scale_table[r:P:16, :], scale_rows[r])
-        wx_sb = sb("wx_sb", [P, 2 * N], U8)
-        nc.sync.dma_start(wx_sb[:].bitcast(I32), wx_words[0].bitcast(I32))
-        x_rows = x.rearrange("(p i) j -> p i j", i=4)
-        x_raw = [sb(f"x_raw{h}", [P, 4, J // 2], F32) for h in range(2)]
-        for q in range(4):
-            nc.sync.dma_start(wx_plane[32 * q : 32 * q + 4, :], wx_scales.bitcast(I32)[0, 4 * q : 4 * q + 4, :])
-            if q == 0:
-                for h in range(2):
-                    nc.sync.dma_start(x_raw[h][:], x_rows[:, :, h * J // 2 : (h + 1) * J // 2])
-        word_table = sb("word_table", [P, T], I32)
-        nc.sync.dma_start(word_table[:], tab_words[0].rearrange("p t c -> p (t c)").bitcast(I32))
-
+        w_planes = sb("w_planes", [P, 2, N // 4], I32)
+        nc.vector.memset(w_planes[:], 0)
         warm = sb("warm", [P, 16], F32)
         nc.vector.memset(warm[:, 0:1], 0.0)
         nc.scalar.activation(warm[:, 8:9], warm[:, 0:1], ACT.Silu)
+        nc.vector.memset(scale_table[0:96, :], 0)
+        tab_planes = [sb(f"tab_plane{a}", [P, G * J // 4], I32) for a in range(2)]
+        for a in range(2):
+            nc.vector.memset(tab_planes[a][:], 0)
 
-        w_sb = sb("w_sb", [P, 2, 2 * N], U8)
-        nc.sync.dma_start(w_sb[:].bitcast(I32), w_words.bitcast(I32).rearrange("a p n -> p a n"))
-        w_planes = sb("w_planes", [P, 2, N // 4], I32)
-        nc.vector.memset(w_planes[:], 0)
+        columns = sb("columns", [P, G + 1, 8], F32)
+
+        def load_column(queue, slot, vec):
+            with nc.allow_non_contiguous_dma(reason="one value a partition"):
+                queue.dma_start(columns[:, slot, 0:JT], vec.rearrange("(t p) -> p t", p=P))
+
+        for q in range(4):
+            nc.sync.dma_start(wx_plane[32 * q : 32 * q + 4, :], wx_scales.bitcast(I32)[0, 4 * q : 4 * q + 4, :])
+        load_column(nc.sync, 0, iw0)
+        x_raw = sb("x_raw", [P, 4, J], F32)
+        nc.sync.dma_start(x_raw[:], x.rearrange("(p i) j -> p i j", i=4))
+        wx_sb = sb("wx_sb", [P, 2 * N], U8)
+        nc.sync.dma_start(wx_sb[:].bitcast(I32), wx_words[0].bitcast(I32))
         for q in range(4):
             nc.sync.dma_start(
                 w_planes[32 * q : 32 * q + 4, :, :],
                 w_scales.bitcast(I32)[:, 4 * q : 4 * q + 4, :].rearrange("a r n -> r a n"),
             )
+        word_table = sb("word_table", [P, T], I32)
+        nc.sync.dma_start(word_table[:], tab_words[0].rearrange("p t c -> p (t c)").bitcast(I32))
+        w_sb = sb("w_sb", [P, 2, 2 * N], U8)
+        nc.sync.dma_start(w_sb[:].bitcast(I32), w_words.bitcast(I32).rearrange("a p n -> p a n"))
 
-        shifted_scales = [sb(f"shifted_scales{h}", [P, 2 * J // 4], I32) for h in range(2)]
-        for h in range(2):
-            nc.vector.memset(shifted_scales[h][96:P, :], 0)
         ident = sb("ident", [P, P], F32)
         nc.vector.memset(ident[:], 0.0)
         make_identity(nc, ident[:], nomemset=True)
+
+        picked_scales = sb("picked_scales", [P, G * J], U8)
+        for g in range(G):
+            nc.vector.tensor_copy(
+                picked_scales[:, g * J : (g + 1) * J],
+                scale_table[:].bitcast(U8).indirect(offsets[:, g * LIST_COLS : (g + 1) * LIST_COLS]),
+            )
+        for a in range(2):
+            for q in (0, 2, 1, 3):
+                row = 96 + 16 * a + 4 * q
+                nc.sync.dma_start(tab_planes[a][32 * q : 32 * q + 4, :], picked_scales[row : row + 4, :].bitcast(I32))
+        for slot, vec in ((1, iw1), (2, iw2), (3, iw3), (4, b)):
+            load_column(nc.sync, slot, vec)
 
         final = [fin_pool.tile([P, NT, P], F32, name=f"final{jt}") for jt in range(JT)]
 
@@ -97,15 +110,14 @@ def tile_list_interp_silu_kernel(
         x_plane = sb("x_plane", [P, J], U8)
         for jt in range(JT):
             cols = slice(jt * P, (jt + 1) * P)
-            h, u = divmod(jt, 2)
             x_bf = sb(f"x_bf{jt}", [P, P, 4], BF16)
-            nc.scalar.copy(x_bf[:], x_raw[h][:, :, u * P : (u + 1) * P].rearrange("p i j -> p j i"))
+            nc.scalar.copy(x_bf[:], x_raw[:, :, cols].rearrange("p i j -> p j i"))
             nc.vector.quantize_mx(
                 out=x_codes[:, cols].bitcast(FP8X4), scales=x_plane[:, cols], in_=x_bf[:].rearrange("p j i -> p (j i)")
             )
         for jt in range(JT):
             cols = slice(jt * P, (jt + 1) * P)
-            bank = acc_pool.tile([P, N], F32, name="bank")
+            bank = acc_pool.tile([P, N], F32, name=f"bank{jt}")
             nc.tensor.matmul_mx(
                 out=bank[:],
                 lhsT=x_codes[:, cols].bitcast(FP8X4),
@@ -119,32 +131,12 @@ def tile_list_interp_silu_kernel(
             nc.scalar.copy(skip[:], bank[:])
             add_transposed(jt, skip, True, False)
 
-        columns = sb("columns", [P, G + 1, 8], F32)
-        picked_scales = [sb("picked_scales0", [P, 2 * J], U8), sb("picked_scales1", [P, 2 * J], U8, tag="x_bf1")]
-
-        def load_column(slot, vec):
-            with nc.allow_non_contiguous_dma(reason="one value a partition"):
-                nc.sync.dma_start(columns[:, slot, 0:JT], vec.rearrange("(t p) -> p t", p=P))
-
-        for g in range(G):
-            h, u = divmod(g, 2)
-            nc.vector.tensor_copy(
-                picked_scales[h][:, u * J : (u + 1) * J],
-                scale_table[:].bitcast(U8).indirect(offsets[:, g * LIST_COLS : (g + 1) * LIST_COLS]),
-            )
-            if u == 1:
-                nc.sync.dma_start(shifted_scales[h][0 : P - 16, :], picked_scales[h][16:P, :].bitcast(I32))
-                if h == 0:
-                    load_column(0, iw0)
-        for slot, vec in ((1, iw1), (2, iw2), (3, iw3), (4, b)):
-            load_column(slot, vec)
-
-        warm_bank = acc_pool.tile([P, N], F32, name="bank")
+        warm_bank = acc_pool.tile([P, N], F32, name="bank3")
         for i in range(2):
             nc.tensor.matmul_mx(
                 out=warm_bank[:],
                 lhsT=wx_sb[:, 0 : 2 * P].bitcast(FP4X4),
-                lhsT_scale=picked_scales[1][:, J : J + P],
+                lhsT_scale=wx_plane[:].bitcast(U8)[:, 0:P],
                 rhs=wx_sb[:].bitcast(FP4X4),
                 rhs_scale=wx_plane[:].bitcast(U8),
                 start=(i == 0),
@@ -166,15 +158,13 @@ def tile_list_interp_silu_kernel(
             parted.append(halves)
 
         def project(g, jt):
-            h, u = divmod(g, 2)
-            bank = acc_pool.tile([P, N], F32, name="bank")
-            c0 = u * J + jt * P
-            planes = (picked_scales[h][:], shifted_scales[h][:].bitcast(U8))
+            bank = acc_pool.tile([P, N], F32, name=f"bank{jt}")
+            c0 = g * J + jt * P
             for a in range(2):
                 nc.tensor.matmul_mx(
                     out=bank[:],
                     lhsT=parted[g][:, a, 2 * jt * P : 2 * (jt + 1) * P].bitcast(FP4X4),
-                    lhsT_scale=planes[a][:, c0 : c0 + P],
+                    lhsT_scale=tab_planes[a][:].bitcast(U8)[:, c0 : c0 + P],
                     rhs=w_sb[:, a, :].bitcast(FP4X4),
                     rhs_scale=w_planes[:, a, :].bitcast(U8),
                     start=(a == 0),

@@ -144,16 +144,18 @@ def tile_list_interp_silu_kernel(
             )
 
         parted = []
+        picked = sb("picked", [P, G * J - (G - 1) * P], U32)
         for g in range(G):
-            picked = sb(f"picked{g}", [P, J], U32)
+            base = (G - 1 - g) * (J - P)
             nc.vector.tensor_copy(
-                picked[:], word_table[:].bitcast(U32).indirect(offsets[:, g * LIST_COLS : (g + 1) * LIST_COLS])
+                picked[:, base : base + J],
+                word_table[:].bitcast(U32).indirect(offsets[:, g * LIST_COLS : (g + 1) * LIST_COLS]),
             )
             halves = sb(f"parted{g}", [P, 2, 2 * J], U8)
-            pieces = (0, P, J) if g < 2 else (0, J)
-            for c0, c1 in zip(pieces, pieces[1:]):
+            for c0, c1 in ((0, P), (P, J)):
                 nc.vector.tensor_copy(
-                    halves[:].bitcast(U16)[:, :, c0:c1], picked[:, c0:c1].bitcast(U16).rearrange("p (j d) -> p d j", d=2)
+                    halves[:].bitcast(U16)[:, :, c0:c1],
+                    picked[:, base + c0 : base + c1].bitcast(U16).rearrange("p (j d) -> p d j", d=2),
                 )
             parted.append(halves)
 
@@ -186,8 +188,8 @@ def tile_list_interp_silu_kernel(
 
         out_view = out.rearrange("(t p) j -> p t j", p=P)
         for jt in range(JT):
-            add_transposed(jt, parts[0, jt], False, False)
-            add_transposed(jt, parts[G - 1, jt], False, True)
+            add_transposed(jt, parts[G - 1, jt], False, False)
+            add_transposed(jt, parts[0, jt], False, True)
             result = sb(f"result{jt}", [P, NT, P], F32)
             for nt in range(NT):
                 nc.scalar.activation(result[:, nt, :], final[jt][:, nt, :], ACT.Silu, bias=columns[:, G, nt : nt + 1])

@@ -93,17 +93,19 @@ def tile_list_interp_silu_kernel(
         for slot, vec in ((1, iw1), (2, iw2), (3, iw3), (4, b)):
             load_column(nc.sync, slot, vec)
 
-        final = [fin_pool.tile([P, NT, P], F32, name=f"final{jt}") for jt in range(JT)]
+        final = [[fin_pool.tile([P, 2, 2 * P], F32, name=f"final{jp}_{half}") for half in range(2)] for jp in range(2)]
 
         def add_transposed(jt, part, first, last):
+            jp, u = divmod(jt, 2)
             for nt in range(NT):
+                half, v = divmod(nt, 2)
                 nc.tensor.matmul(
-                    final[jt][:, nt, :],
+                    final[jp][half][:, v, u * P : (u + 1) * P],
                     lhsT=part[:, nt * P : (nt + 1) * P],
                     rhs=ident[:],
                     is_transpose=True,
-                    start=(first and nt == 0),
-                    stop=(last and nt == NT - 1),
+                    start=(first and v == 0),
+                    stop=(last and v == 1),
                 )
 
         x_codes = sb("x_codes", [P, J], U32)
@@ -129,7 +131,7 @@ def tile_list_interp_silu_kernel(
             )
             skip = sb(f"skip{jt}", [P, N], F32)
             nc.scalar.copy(skip[:], bank[:])
-            add_transposed(jt, skip, True, False)
+            add_transposed(jt, skip, jt % 2 == 0, False)
 
         warm_bank = acc_pool.tile([P, N], F32, name="bank3")
         for i in range(2):
@@ -187,11 +189,13 @@ def tile_list_interp_silu_kernel(
                 parts[g, jt] = part
 
         out_view = out.rearrange("(t p) j -> p t j", p=P)
-        for jt in range(JT):
-            add_transposed(jt, parts[G - 1, jt], False, False)
-            add_transposed(jt, parts[0, jt], False, True)
-            result = sb(f"result{jt}", [P, NT, P], F32)
+        for jp in range(2):
+            add_transposed(2 * jp, parts[G - 1, 2 * jp], False, False)
+            add_transposed(2 * jp, parts[0, 2 * jp], False, False)
+            add_transposed(2 * jp + 1, parts[0, 2 * jp + 1], False, False)
+            add_transposed(2 * jp + 1, parts[G - 1, 2 * jp + 1], False, True)
             for nt in range(NT):
-                nc.scalar.activation(result[:, nt, :], final[jt][:, nt, :], ACT.Silu, bias=columns[:, G, nt : nt + 1])
-                if nt % 2 == 1:
-                    nc.sync.dma_start(out_view[:, nt - 1 : nt + 1, jt * P : (jt + 1) * P], result[:, nt - 1 : nt + 1, :])
+                half, v = divmod(nt, 2)
+                result = sb(f"result{jp}_{nt}", [P, 2 * P], F32)
+                nc.scalar.activation(result[:], final[jp][half][:, v, :], ACT.Silu, bias=columns[:, G, nt : nt + 1])
+                nc.sync.dma_start(out_view[:, nt, 2 * jp * P : 2 * (jp + 1) * P], result[:])

@@ -95,10 +95,10 @@ def tile_list_interp_silu_kernel(
 
         final = [[fin_pool.tile([P, 2, 2 * P], F32, name=f"final{jp}_{half}") for half in range(2)] for jp in range(2)]
 
-        def add_transposed(jt, part, first, last):
+        def add_transposed(jt, half, part, first, last):
             jp, u = divmod(jt, 2)
-            for nt in range(NT):
-                half, v = divmod(nt, 2)
+            for v in range(2):
+                nt = 2 * half + v
                 nc.tensor.matmul(
                     final[jp][half][:, v, u * P : (u + 1) * P],
                     lhsT=part[:, nt * P : (nt + 1) * P],
@@ -131,7 +131,8 @@ def tile_list_interp_silu_kernel(
             )
             skip = sb(f"skip{jt}", [P, N], F32)
             nc.scalar.copy(skip[:], bank[:])
-            add_transposed(jt, skip, jt % 2 == 0, False)
+            for half in range(2):
+                add_transposed(jt, half, skip, jt % 2 == 0, False)
 
         warm_bank = acc_pool.tile([P, N], F32, name="bank3")
         for i in range(2):
@@ -190,12 +191,13 @@ def tile_list_interp_silu_kernel(
 
         out_view = out.rearrange("(t p) j -> p t j", p=P)
         for jp in range(2):
-            add_transposed(2 * jp, parts[G - 1, 2 * jp], False, False)
-            add_transposed(2 * jp, parts[0, 2 * jp], False, False)
-            add_transposed(2 * jp + 1, parts[0, 2 * jp + 1], False, False)
-            add_transposed(2 * jp + 1, parts[G - 1, 2 * jp + 1], False, True)
-            for nt in range(NT):
-                half, v = divmod(nt, 2)
-                result = sb(f"result{jp}_{nt}", [P, 2 * P], F32)
-                nc.scalar.activation(result[:], final[jp][half][:, v, :], ACT.Silu, bias=columns[:, G, nt : nt + 1])
-                nc.sync.dma_start(out_view[:, nt, 2 * jp * P : 2 * (jp + 1) * P], result[:])
+            for half in range(2):
+                add_transposed(2 * jp, half, parts[G - 1, 2 * jp], False, False)
+                add_transposed(2 * jp, half, parts[0, 2 * jp], False, False)
+                add_transposed(2 * jp + 1, half, parts[0, 2 * jp + 1], False, False)
+                add_transposed(2 * jp + 1, half, parts[G - 1, 2 * jp + 1], False, True)
+                for v in range(2):
+                    nt = 2 * half + v
+                    result = sb(f"result{jp}_{nt}", [P, 2 * P], F32)
+                    nc.scalar.activation(result[:], final[jp][half][:, v, :], ACT.Silu, bias=columns[:, G, nt : nt + 1])
+                    nc.sync.dma_start(out_view[:, nt, 2 * jp * P : 2 * (jp + 1) * P], result[:])

@@ -22,6 +22,7 @@ ALU = mybir.AluOpType
 JT = J // P
 NT = N // P
 LIST_COLS = J // 16
+CUTS = (0, 512, 1152, 2048)
 
 
 def tile_list_interp_silu_kernel(
@@ -34,7 +35,7 @@ def tile_list_interp_silu_kernel(
         fin_pool = ctx.enter_context(tc.psum_pool(name="fin", bufs=1))
 
         def sb(name, shape, dtype, tag=None):
-            return held.tile(shape, dtype, name=name, tag=tag or name, align_bytes=64)
+            return held.tile(shape, dtype, name=name, tag=tag or name, align_bytes=256)
 
         offsets = held.tile([P, G * LIST_COLS], U16, name="offsets")
         nc.sync.dma_start(offsets[:], offs)
@@ -134,33 +135,25 @@ def tile_list_interp_silu_kernel(
             for half in range(2):
                 add_transposed(jt, half, skip, jt % 2 == 0, False)
 
-        warm_bank = acc_pool.tile([P, N], F32, name="bank3")
-        for i in range(2):
-            nc.tensor.matmul_mx(
-                out=warm_bank[:],
-                lhsT=wx_sb[:, 0 : 2 * P].bitcast(FP4X4),
-                lhsT_scale=wx_plane[:].bitcast(U8)[:, 0:P],
-                rhs=wx_sb[:].bitcast(FP4X4),
-                rhs_scale=wx_plane[:].bitcast(U8),
-                start=(i == 0),
-                stop=(i == 1),
-            )
-
-        parted = []
-        picked = sb("picked", [P, G * J - (G - 1) * P], U32)
-        for g in range(G):
-            base = (G - 1 - g) * (J - P)
+        entries = G * J
+        parted = {}
+        picked = sb("picked", [P, entries - (len(CUTS) - 2) * P], U32)
+        top = entries - (len(CUTS) - 2) * P
+        for e0, e1 in zip(CUTS, CUTS[1:]):
+            base = top - (e1 - e0)
+            top = base + P
             nc.vector.tensor_copy(
-                picked[:, base : base + J],
-                word_table[:].bitcast(U32).indirect(offsets[:, g * LIST_COLS : (g + 1) * LIST_COLS]),
+                picked[:, base : base + e1 - e0], word_table[:].bitcast(U32).indirect(offsets[:, e0 // 16 : e1 // 16])
             )
-            halves = sb(f"parted{g}", [P, 2, 2 * J], U8)
-            for c0, c1 in ((0, P), (P, J)):
+            pieces = sorted({e0, e0 + P, e1} | {e for e in range(0, entries, J) if e0 < e < e1})
+            for c0, c1 in zip(pieces, pieces[1:]):
+                piece = sb(f"parted{c0}", [P, 2, 2 * (c1 - c0)], U8)
+                for c in range(c0, c1, P):
+                    parted[c] = piece[:, :, 2 * (c - c0) : 2 * (c - c0 + P)]
                 nc.vector.tensor_copy(
-                    halves[:].bitcast(U16)[:, :, c0:c1],
-                    picked[:, base + c0 : base + c1].bitcast(U16).rearrange("p (j d) -> p d j", d=2),
+                    piece[:].bitcast(U16),
+                    picked[:, base + c0 - e0 : base + c1 - e0].bitcast(U16).rearrange("p (j d) -> p d j", d=2),
                 )
-            parted.append(halves)
 
         def project(g, jt):
             bank = acc_pool.tile([P, N], F32, name=f"bank{jt}")
@@ -168,7 +161,7 @@ def tile_list_interp_silu_kernel(
             for a in range(2):
                 nc.tensor.matmul_mx(
                     out=bank[:],
-                    lhsT=parted[g][:, a, 2 * jt * P : 2 * (jt + 1) * P].bitcast(FP4X4),
+                    lhsT=parted[c0][:, a, :].bitcast(FP4X4),
                     lhsT_scale=tab_planes[a][:].bitcast(U8)[:, c0 : c0 + P],
                     rhs=w_sb[:, a, :].bitcast(FP4X4),
                     rhs_scale=w_planes[:, a, :].bitcast(U8),

@@ -23,6 +23,7 @@ JT = J // P
 NT = N // P
 LIST_COLS = J // 16
 CUTS = (0, 512, 1152, 2048)
+PAIR = 2 * J
 
 
 def tile_list_interp_silu_kernel(
@@ -31,8 +32,7 @@ def tile_list_interp_silu_kernel(
     nc = tc.nc
     with ExitStack() as ctx:
         held = ctx.enter_context(tc.tile_pool(name="held", bufs=1))
-        acc_pool = ctx.enter_context(tc.psum_pool(name="acc", bufs=1))
-        fin_pool = ctx.enter_context(tc.psum_pool(name="fin", bufs=1))
+        psum = ctx.enter_context(tc.psum_pool(name="psum", bufs=1))
 
         def sb(name, shape, dtype, tag=None):
             return held.tile(shape, dtype, name=name, tag=tag or name, align_bytes=256)
@@ -42,31 +42,22 @@ def tile_list_interp_silu_kernel(
 
         scale_table = sb("scale_table", [P, T // 4], I32)
         nc.sync.dma_start(scale_table[96:P, :], tab_scales.bitcast(I32).rearrange("a q t -> (a q) t"))
-        wx_plane = sb("wx_plane", [P, N // 4], I32)
-        nc.vector.memset(wx_plane[:], 0)
         w_planes = sb("w_planes", [P, 2, N // 4], I32)
-        nc.vector.memset(w_planes[:], 0)
+        nc.gpsimd.memset(w_planes[:], 0)
+        nc.vector.memset(scale_table[0:96, :], 0)
         warm = sb("warm", [P, 16], F32)
         nc.vector.memset(warm[:, 0:1], 0.0)
         nc.scalar.activation(warm[:, 8:9], warm[:, 0:1], ACT.Silu)
-        nc.vector.memset(scale_table[0:96, :], 0)
-        tab_planes = [sb(f"tab_plane{a}", [P, G * J // 4], I32) for a in range(2)]
+        tab_planes = [[sb(f"tab_plane{h}_{a}", [P, PAIR // 4], I32) for a in range(2)] for h in range(2)]
         for a in range(2):
-            nc.vector.memset(tab_planes[a][:], 0)
+            nc.vector.memset(tab_planes[0][a][:], 0)
+        for a in range(2):
+            nc.gpsimd.memset(tab_planes[1][a][:], 0)
+        wx_plane = sb("wx_plane", [P, N // 4], I32)
+        nc.gpsimd.memset(wx_plane[:], 0)
 
-        columns = sb("columns", [P, G + 1, 8], F32)
-
-        def load_column(queue, slot, vec):
-            with nc.allow_non_contiguous_dma(reason="one value a partition"):
-                queue.dma_start(columns[:, slot, 0:JT], vec.rearrange("(t p) -> p t", p=P))
-
-        for q in range(4):
-            nc.sync.dma_start(wx_plane[32 * q : 32 * q + 4, :], wx_scales.bitcast(I32)[0, 4 * q : 4 * q + 4, :])
-        load_column(nc.sync, 0, iw0)
-        x_raw = sb("x_raw", [P, 4, J], F32)
-        nc.sync.dma_start(x_raw[:], x.rearrange("(p i) j -> p i j", i=4))
-        wx_sb = sb("wx_sb", [P, 2 * N], U8)
-        nc.sync.dma_start(wx_sb[:].bitcast(I32), wx_words[0].bitcast(I32))
+        w_sb = sb("w_sb", [P, 2, 2 * N], U8)
+        nc.sync.dma_start(w_sb[:].bitcast(I32), w_words.bitcast(I32).rearrange("a p n -> p a n"))
         for q in range(4):
             nc.sync.dma_start(
                 w_planes[32 * q : 32 * q + 4, :, :],
@@ -74,66 +65,43 @@ def tile_list_interp_silu_kernel(
             )
         word_table = sb("word_table", [P, T], I32)
         nc.sync.dma_start(word_table[:], tab_words[0].rearrange("p t c -> p (t c)").bitcast(I32))
-        w_sb = sb("w_sb", [P, 2, 2 * N], U8)
-        nc.sync.dma_start(w_sb[:].bitcast(I32), w_words.bitcast(I32).rearrange("a p n -> p a n"))
+
+        columns = [sb(f"column{slot}", [P, JT], F32) for slot in range(G + 1)]
+
+        def load_column(queue, slot, vec):
+            with nc.allow_non_contiguous_dma(reason="one value a partition"):
+                queue.dma_start(columns[slot][:], vec.rearrange("(t p) -> p t", p=P))
+
+        load_column(nc.gpsimd, 0, iw0)
+        load_column(nc.gpsimd, 1, iw1)
 
         ident = sb("ident", [P, P], F32)
-        nc.vector.memset(ident[:], 0.0)
-        make_identity(nc, ident[:], nomemset=True)
+        make_identity(nc, ident[:])
 
-        picked_scales = sb("picked_scales", [P, G * J], U8)
-        for g in range(G):
+        def move_scales(h):
+            picked_scales = sb(f"picked_scales{h}", [P, PAIR], U8)
             nc.vector.tensor_copy(
-                picked_scales[:, g * J : (g + 1) * J],
-                scale_table[:].bitcast(U8).indirect(offsets[:, g * LIST_COLS : (g + 1) * LIST_COLS]),
+                picked_scales[:],
+                scale_table[:].bitcast(U8).indirect(offsets[:, 2 * h * LIST_COLS : 2 * (h + 1) * LIST_COLS]),
             )
-        for a in range(2):
             for q in (0, 2, 1, 3):
-                row = 96 + 16 * a + 4 * q
-                nc.sync.dma_start(tab_planes[a][32 * q : 32 * q + 4, :], picked_scales[row : row + 4, :].bitcast(I32))
-        for slot, vec in ((1, iw1), (2, iw2), (3, iw3), (4, b)):
-            load_column(nc.sync, slot, vec)
+                for a in range(2):
+                    row = 96 + 16 * a + 4 * q
+                    nc.sync.dma_start(
+                        tab_planes[h][a][32 * q : 32 * q + 4, :], picked_scales[row : row + 4, :].bitcast(I32)
+                    )
 
-        final = [[fin_pool.tile([P, 2, 2 * P], F32, name=f"final{jp}_{half}") for half in range(2)] for jp in range(2)]
-
-        def add_transposed(jt, half, part, first, last):
-            jp, u = divmod(jt, 2)
-            for v in range(2):
-                nt = 2 * half + v
-                nc.tensor.matmul(
-                    final[jp][half][:, v, u * P : (u + 1) * P],
-                    lhsT=part[:, nt * P : (nt + 1) * P],
-                    rhs=ident[:],
-                    is_transpose=True,
-                    start=(first and v == 0),
-                    stop=(last and v == 1),
-                )
-
-        x_codes = sb("x_codes", [P, J], U32)
-        x_plane = sb("x_plane", [P, J], U8)
-        for jt in range(JT):
-            cols = slice(jt * P, (jt + 1) * P)
-            x_bf = sb(f"x_bf{jt}", [P, P, 4], BF16)
-            nc.scalar.copy(x_bf[:], x_raw[:, :, cols].rearrange("p i j -> p j i"))
-            nc.vector.quantize_mx(
-                out=x_codes[:, cols].bitcast(FP8X4), scales=x_plane[:, cols], in_=x_bf[:].rearrange("p j i -> p (j i)")
-            )
-        for jt in range(JT):
-            cols = slice(jt * P, (jt + 1) * P)
-            bank = acc_pool.tile([P, N], F32, name=f"bank{jt}")
-            nc.tensor.matmul_mx(
-                out=bank[:],
-                lhsT=x_codes[:, cols].bitcast(FP8X4),
-                lhsT_scale=x_plane[:, cols],
-                rhs=wx_sb[:].bitcast(FP4X4),
-                rhs_scale=wx_plane[:].bitcast(U8),
-                start=True,
-                stop=True,
-            )
-            skip = sb(f"skip{jt}", [P, N], F32)
-            nc.scalar.copy(skip[:], bank[:])
-            for half in range(2):
-                add_transposed(jt, half, skip, jt % 2 == 0, False)
+        move_scales(0)
+        x_raw = sb("x_raw", [P, 4, J], F32)
+        nc.sync.dma_start(x_raw[:], x.rearrange("(p i) j -> p i j", i=4))
+        move_scales(1)
+        load_column(nc.sync, 2, iw2)
+        load_column(nc.sync, 3, iw3)
+        wx_sb = sb("wx_sb", [P, 2 * N], U8)
+        nc.sync.dma_start(wx_sb[:].bitcast(I32), wx_words[0].bitcast(I32))
+        for q in range(4):
+            nc.sync.dma_start(wx_plane[32 * q : 32 * q + 4, :], wx_scales.bitcast(I32)[0, 4 * q : 4 * q + 4, :])
+        load_column(nc.sync, 4, b)
 
         entries = G * J
         parted = {}
@@ -156,13 +124,13 @@ def tile_list_interp_silu_kernel(
                 )
 
         def project(g, jt):
-            bank = acc_pool.tile([P, N], F32, name=f"bank{jt}")
+            bank = psum.tile([P, N], F32, name=f"acc{g}_{jt}", tag=f"bank{JT * (g % 2) + jt}")
             c0 = g * J + jt * P
             for a in range(2):
                 nc.tensor.matmul_mx(
                     out=bank[:],
                     lhsT=parted[c0][:, a, :].bitcast(FP4X4),
-                    lhsT_scale=tab_planes[a][:].bitcast(U8)[:, c0 : c0 + P],
+                    lhsT_scale=tab_planes[g // 2][a][:].bitcast(U8)[:, c0 % PAIR : c0 % PAIR + P],
                     rhs=w_sb[:, a, :].bitcast(FP4X4),
                     rhs_scale=w_planes[:, a, :].bitcast(U8),
                     start=(a == 0),
@@ -171,26 +139,82 @@ def tile_list_interp_silu_kernel(
             return bank
 
         parts = {}
-        for g in range(G):
+
+        def neighbour(g):
             for jt in range(JT):
                 bank = project(g, jt)
                 part = sb(f"part{g}_{jt}", [P, N], F32)
-                weight = columns[:, g, jt : jt + 1]
+                weight = columns[g][:, jt : jt + 1]
                 if g < 2:
                     nc.scalar.activation(part[:], bank[:], ACT.Copy, scale=weight)
                 else:
                     nc.vector.scalar_tensor_tensor(part[:], bank[:], weight, parts[g - 1, jt][:], ALU.mult, ALU.add)
                 parts[g, jt] = part
 
+        for g in range(G - 1):
+            neighbour(g)
+
+        x_codes = sb("x_codes", [P, J], U32, tag=f"part1_{JT - 1}")
+        x_plane = sb("x_plane", [P, J], U8)
+        for jp in range(2):
+            cols = slice(2 * jp * P, 2 * (jp + 1) * P)
+            x_bf = sb(f"x_bf{jp}", [P, 2 * P, 4], BF16)
+            nc.scalar.copy(x_bf[:], x_raw[:, :, cols].rearrange("p i j -> p j i"))
+            nc.vector.quantize_mx(
+                out=x_codes[:, cols].bitcast(FP8X4), scales=x_plane[:, cols], in_=x_bf[:].rearrange("p j i -> p (j i)")
+            )
+        neighbour(G - 1)
+
+        final = [
+            [psum.tile([P, 2, 2 * P], F32, name=f"final{jp}_{half}", tag=f"bank{2 * jp + half}") for half in range(2)]
+            for jp in range(2)
+        ]
+
+        def add_transposed(jt, half, part, first, last):
+            jp, u = divmod(jt, 2)
+            for v in range(2):
+                nt = 2 * half + v
+                nc.tensor.matmul(
+                    final[jp][half][:, v, u * P : (u + 1) * P],
+                    lhsT=part[:, nt * P : (nt + 1) * P],
+                    rhs=ident[:],
+                    is_transpose=True,
+                    start=(first and v == 0),
+                    stop=(last and v == 1),
+                )
+
+        for jp in range(2):
+            for half in range(2):
+                for u in range(2):
+                    add_transposed(2 * jp + u, half, parts[0, 2 * jp + u], u == 0, False)
+
+        total = {}
+        skips = {}
+        for jt in range(JT):
+            cols = slice(jt * P, (jt + 1) * P)
+            bank = psum.tile([P, N], F32, name=f"skip{jt}", tag=f"bank{JT + jt}")
+            nc.tensor.matmul_mx(
+                out=bank[:],
+                lhsT=x_codes[:, cols].bitcast(FP8X4),
+                lhsT_scale=x_plane[:, cols],
+                rhs=wx_sb[:].bitcast(FP4X4),
+                rhs_scale=wx_plane[:].bitcast(U8),
+                start=True,
+                stop=True,
+            )
+            skips[jt] = bank
+            total[jt] = sb(f"total{jt}", [P, N], F32)
+
         out_view = out.rearrange("(t p) j -> p t j", p=P)
         for jp in range(2):
             for half in range(2):
-                add_transposed(2 * jp, half, parts[G - 1, 2 * jp], False, False)
-                add_transposed(2 * jp, half, parts[0, 2 * jp], False, False)
-                add_transposed(2 * jp + 1, half, parts[0, 2 * jp + 1], False, False)
-                add_transposed(2 * jp + 1, half, parts[G - 1, 2 * jp + 1], False, True)
+                chans = slice(half * N // 2, (half + 1) * N // 2)
+                for jt in (2 * jp, 2 * jp + 1):
+                    nc.vector.tensor_tensor(total[jt][:, chans], skips[jt][:, chans], parts[G - 1, jt][:, chans], ALU.add)
+                add_transposed(2 * jp, half, total[2 * jp], False, False)
+                add_transposed(2 * jp + 1, half, total[2 * jp + 1], False, True)
                 for v in range(2):
                     nt = 2 * half + v
                     result = sb(f"result{jp}_{nt}", [P, 2 * P], F32)
-                    nc.scalar.activation(result[:], final[jp][half][:, v, :], ACT.Silu, bias=columns[:, G, nt : nt + 1])
+                    nc.scalar.activation(result[:], final[jp][half][:, v, :], ACT.Silu, bias=columns[G][:, nt : nt + 1])
                     nc.sync.dma_start(out_view[:, nt, 2 * jp * P : 2 * (jp + 1) * P], result[:])

@@ -38,10 +38,9 @@ def tile_list_interp_silu_kernel(
             return held.tile(shape, dtype, name=name, tag=tag or name, align_bytes=256)
 
         offsets = held.tile([P, G * LIST_COLS], U16, name="offsets")
-        nc.sync.dma_start(offsets[:], offs)
-
         scale_table = sb("scale_table", [P, T // 4], I32)
         nc.sync.dma_start(scale_table[96:P, :], tab_scales.bitcast(I32).rearrange("a q t -> (a q) t"))
+        nc.sync.dma_start(offsets[:], offs)
         w_planes = sb("w_planes", [P, 2, N // 4], I32)
         nc.gpsimd.memset(w_planes[:], 0)
         nc.vector.memset(scale_table[0:96, :], 0)
@@ -72,8 +71,6 @@ def tile_list_interp_silu_kernel(
             with nc.allow_non_contiguous_dma(reason="one value a partition"):
                 queue.dma_start(columns[slot][:], vec.rearrange("(t p) -> p t", p=P))
 
-        load_column(nc.gpsimd, 0, iw0)
-        load_column(nc.gpsimd, 1, iw1)
 
         ident = sb("ident", [P, P], F32)
         make_identity(nc, ident[:])
@@ -87,11 +84,14 @@ def tile_list_interp_silu_kernel(
             for q in (0, 2, 1, 3):
                 for a in range(2):
                     row = 96 + 16 * a + 4 * q
-                    nc.sync.dma_start(
+                    queue = nc.gpsimd if (h, q, a) == (0, 0, 1) else nc.sync
+                    queue.dma_start(
                         tab_planes[h][a][32 * q : 32 * q + 4, :], picked_scales[row : row + 4, :].bitcast(I32)
                     )
 
         move_scales(0)
+        load_column(nc.sync, 0, iw0)
+        load_column(nc.sync, 1, iw1)
         x_raw = sb("x_raw", [P, 4, J], F32)
         nc.sync.dma_start(x_raw[:], x.rearrange("(p i) j -> p i j", i=4))
         move_scales(1)
@@ -122,6 +122,18 @@ def tile_list_interp_silu_kernel(
                     piece[:].bitcast(U16),
                     picked[:, base + c0 - e0 : base + c1 - e0].bitcast(U16).rearrange("p (j d) -> p d j", d=2),
                 )
+
+        warm_bank = psum.tile([P, N], F32, name="warm_bank", tag=f"bank{2 * JT - 1}")
+        for r in range(3):
+            nc.tensor.matmul_mx(
+                out=warm_bank[:],
+                lhsT=word_table[:, 0 : P // 2].bitcast(FP4X4),
+                lhsT_scale=w_planes[:, 1, :].bitcast(U8)[:, 0:P],
+                rhs=w_sb[:, 0, :].bitcast(FP4X4),
+                rhs_scale=w_planes[:, 0, :].bitcast(U8),
+                start=True,
+                stop=True,
+            )
 
         def project(g, jt):
             bank = psum.tile([P, N], F32, name=f"acc{g}_{jt}", tag=f"bank{JT * (g % 2) + jt}")

@@ -22,7 +22,6 @@ ALU = mybir.AluOpType
 JT = J // P
 NT = N // P
 LIST_COLS = J // 16
-CUTS = (0, 512, 1152, 2048)
 PAIR = 2 * J
 
 
@@ -65,15 +64,25 @@ def tile_list_interp_silu_kernel(
         word_table = sb("word_table", [P, T], I32)
         nc.sync.dma_start(word_table[:], tab_words[0].rearrange("p t c -> p (t c)").bitcast(I32))
 
-        columns = [sb(f"column{slot}", [P, JT], F32) for slot in range(G + 1)]
+        columns = {slot: sb(f"column{slot}", [P, JT], F32)[:] for slot in range(2, G + 1)}
 
         def load_column(queue, slot, vec):
             with nc.allow_non_contiguous_dma(reason="one value a partition"):
-                queue.dma_start(columns[slot][:], vec.rearrange("(t p) -> p t", p=P))
+                queue.dma_start(columns[slot], vec.rearrange("(t p) -> p t", p=P))
 
 
         ident = sb("ident", [P, P], F32)
         make_identity(nc, ident[:])
+        rows = sb("rows", [P, P], F32)
+        nc.gpsimd.memset(rows[:], 0.0)
+        for slot, vec in enumerate((iw0, iw1)):
+            nc.gpsimd.dma_start(rows[JT * slot : JT * (slot + 1), :], vec.rearrange("(t p) -> t p", p=P))
+        turned = psum.tile([P, P], F32, name="turned", tag=f"bank{2 * JT - 1}")
+        nc.tensor.matmul(turned[:], lhsT=rows[:], rhs=ident[:], is_transpose=True, start=True, stop=True)
+        early = sb("early", [P, 2 * JT], F32)
+        nc.scalar.copy(early[:], turned[:, 0 : 2 * JT])
+        for slot in range(2):
+            columns[slot] = early[:, JT * slot : JT * (slot + 1)]
 
         def move_scales(h):
             picked_scales = sb(f"picked_scales{h}", [P, PAIR], U8)
@@ -82,16 +91,14 @@ def tile_list_interp_silu_kernel(
                 scale_table[:].bitcast(U8).indirect(offsets[:, 2 * h * LIST_COLS : 2 * (h + 1) * LIST_COLS]),
             )
             for q in (0, 2, 1, 3):
-                for a in range(2):
+                for a in (1, 0):
                     row = 96 + 16 * a + 4 * q
-                    queue = nc.gpsimd if (h, q, a) == (0, 0, 1) else nc.sync
+                    queue = nc.gpsimd if (q, a) == (0, 1) else nc.sync
                     queue.dma_start(
                         tab_planes[h][a][32 * q : 32 * q + 4, :], picked_scales[row : row + 4, :].bitcast(I32)
                     )
 
         move_scales(0)
-        load_column(nc.sync, 0, iw0)
-        load_column(nc.sync, 1, iw1)
         x_raw = sb("x_raw", [P, 4, J], F32)
         nc.sync.dma_start(x_raw[:], x.rearrange("(p i) j -> p i j", i=4))
         move_scales(1)
@@ -103,25 +110,29 @@ def tile_list_interp_silu_kernel(
             nc.sync.dma_start(wx_plane[32 * q : 32 * q + 4, :], wx_scales.bitcast(I32)[0, 4 * q : 4 * q + 4, :])
         load_column(nc.sync, 4, b)
 
-        entries = G * J
         parted = {}
-        picked = sb("picked", [P, entries - (len(CUTS) - 2) * P], U32)
-        top = entries - (len(CUTS) - 2) * P
-        for e0, e1 in zip(CUTS, CUTS[1:]):
-            base = top - (e1 - e0)
-            top = base + P
+        picked = sb("picked", [P, G * J - (G - 1) * P], U32)
+
+        def part_words(g, j0, j1):
+            base = (G - 1 - g) * (J - P)
+            piece = sb(f"parted{g * J + j0}", [P, 2, 2 * (j1 - j0)], U8)
+            for j in range(j0, j1, P):
+                parted[g * J + j] = piece[:, :, 2 * (j - j0) : 2 * (j - j0 + P)]
             nc.vector.tensor_copy(
-                picked[:, base : base + e1 - e0], word_table[:].bitcast(U32).indirect(offsets[:, e0 // 16 : e1 // 16])
+                piece[:].bitcast(U16),
+                picked[:, base + j0 : base + j1].bitcast(U16).rearrange("p (j d) -> p d j", d=2),
             )
-            pieces = sorted({e0, e0 + P, e1} | {e for e in range(0, entries, J) if e0 < e < e1})
-            for c0, c1 in zip(pieces, pieces[1:]):
-                piece = sb(f"parted{c0}", [P, 2, 2 * (c1 - c0)], U8)
-                for c in range(c0, c1, P):
-                    parted[c] = piece[:, :, 2 * (c - c0) : 2 * (c - c0 + P)]
-                nc.vector.tensor_copy(
-                    piece[:].bitcast(U16),
-                    picked[:, base + c0 - e0 : base + c1 - e0].bitcast(U16).rearrange("p (j d) -> p d j", d=2),
-                )
+
+        for g in range(G):
+            base = (G - 1 - g) * (J - P)
+            nc.vector.tensor_copy(
+                picked[:, base : base + J],
+                word_table[:].bitcast(U32).indirect(offsets[:, g * LIST_COLS : (g + 1) * LIST_COLS]),
+            )
+            if g > 0:
+                part_words(g - 1, J - P, J)
+            part_words(g, 0, P)
+            part_words(g, P, J - P if g < G - 1 else J)
 
         warm_bank = psum.tile([P, N], F32, name="warm_bank", tag=f"bank{2 * JT - 1}")
         for r in range(3):
@@ -166,7 +177,7 @@ def tile_list_interp_silu_kernel(
         for g in range(G - 1):
             neighbour(g)
 
-        x_codes = sb("x_codes", [P, J], U32, tag=f"part1_{JT - 1}")
+        x_codes = sb("x_codes", [P, J], U32, tag=f"part1_{JT - 2}")
         x_plane = sb("x_plane", [P, J], U8)
         for jp in range(2):
             cols = slice(2 * jp * P, 2 * (jp + 1) * P)
@@ -178,7 +189,7 @@ def tile_list_interp_silu_kernel(
         neighbour(G - 1)
 
         final = [
-            [psum.tile([P, 2, 2 * P], F32, name=f"final{jp}_{half}", tag=f"bank{2 * jp + half}") for half in range(2)]
+            [psum.tile([P, 2, 2 * P], F32, name=f"final{jp}_{half}", tag=f"bank{JT + 2 * jp + half}") for half in range(2)]
             for jp in range(2)
         ]
 
@@ -195,16 +206,11 @@ def tile_list_interp_silu_kernel(
                     stop=(last and v == 1),
                 )
 
-        for jp in range(2):
-            for half in range(2):
-                for u in range(2):
-                    add_transposed(2 * jp + u, half, parts[0, 2 * jp + u], u == 0, False)
-
         total = {}
         skips = {}
         for jt in range(JT):
             cols = slice(jt * P, (jt + 1) * P)
-            bank = psum.tile([P, N], F32, name=f"skip{jt}", tag=f"bank{JT + jt}")
+            bank = psum.tile([P, N], F32, name=f"skip{jt}", tag=f"bank{jt}")
             nc.tensor.matmul_mx(
                 out=bank[:],
                 lhsT=x_codes[:, cols].bitcast(FP8X4),
@@ -216,13 +222,22 @@ def tile_list_interp_silu_kernel(
             )
             skips[jt] = bank
             total[jt] = sb(f"total{jt}", [P, N], F32)
+            if jt < 2:
+                nc.scalar.copy(total[jt][:], bank[:])
 
         out_view = out.rearrange("(t p) j -> p t j", p=P)
         for jp in range(2):
             for half in range(2):
                 chans = slice(half * N // 2, (half + 1) * N // 2)
+                for u in range(2):
+                    add_transposed(2 * jp + u, half, parts[0, 2 * jp + u], u == 0, False)
                 for jt in (2 * jp, 2 * jp + 1):
-                    nc.vector.tensor_tensor(total[jt][:, chans], skips[jt][:, chans], parts[G - 1, jt][:, chans], ALU.add)
+                    if jp == 0:
+                        add_transposed(jt, half, parts[G - 1, jt], False, False)
+                    else:
+                        nc.vector.tensor_tensor(
+                            total[jt][:, chans], skips[jt][:, chans], parts[G - 1, jt][:, chans], ALU.add
+                        )
                 add_transposed(2 * jp, half, total[2 * jp], False, False)
                 add_transposed(2 * jp + 1, half, total[2 * jp + 1], False, True)
                 for v in range(2):

@@ -77,7 +77,7 @@ def tile_list_interp_silu_kernel(
         nc.gpsimd.memset(rows[:], 0.0)
         for slot, vec in enumerate((iw0, iw1)):
             nc.gpsimd.dma_start(rows[JT * slot : JT * (slot + 1), :], vec.rearrange("(t p) -> t p", p=P))
-        turned = psum.tile([P, P], F32, name="turned", tag=f"bank{2 * JT - 1}")
+        turned = psum.tile([P, P], F32, name="turned", tag=f"bank{2 * JT - 2}")
         nc.tensor.matmul(turned[:], lhsT=rows[:], rhs=ident[:], is_transpose=True, start=True, stop=True)
         early = sb("early", [P, 2 * JT], F32)
         nc.scalar.copy(early[:], turned[:, 0 : 2 * JT])
@@ -86,22 +86,23 @@ def tile_list_interp_silu_kernel(
 
         def move_scales(h):
             picked_scales = sb(f"picked_scales{h}", [P, PAIR], U8)
-            nc.vector.tensor_copy(
-                picked_scales[:],
-                scale_table[:].bitcast(U8).indirect(offsets[:, 2 * h * LIST_COLS : 2 * (h + 1) * LIST_COLS]),
-            )
-            for q in (0, 2, 1, 3):
-                for a in (1, 0):
-                    row = 96 + 16 * a + 4 * q
-                    queue = nc.gpsimd if (q, a) == (0, 1) else nc.sync
-                    queue.dma_start(
-                        tab_planes[h][a][32 * q : 32 * q + 4, :], picked_scales[row : row + 4, :].bitcast(I32)
-                    )
+            for u in range(2):
+                g = 2 * h + u
+                nc.vector.tensor_copy(
+                    picked_scales[:, u * J : (u + 1) * J],
+                    scale_table[:].bitcast(U8).indirect(offsets[:, g * LIST_COLS : (g + 1) * LIST_COLS]),
+                )
+            order = [(q, a) for q in (0, 2, 1, 3) for a in (1, 0)]
+            for q, a in order:
+                row = 96 + 16 * a + 4 * q
+                queue = nc.gpsimd if (h, q, a) == (1, 0, 1) else nc.sync
+                queue.dma_start(tab_planes[h][a][32 * q : 32 * q + 4, :], picked_scales[row : row + 4, :].bitcast(I32))
+            return picked_scales
 
         move_scales(0)
         x_raw = sb("x_raw", [P, 4, J], F32)
         nc.sync.dma_start(x_raw[:], x.rearrange("(p i) j -> p i j", i=4))
-        move_scales(1)
+        late_scales = move_scales(1)
         load_column(nc.sync, 2, iw2)
         load_column(nc.sync, 3, iw3)
         wx_sb = sb("wx_sb", [P, 2 * N], U8)
@@ -138,8 +139,8 @@ def tile_list_interp_silu_kernel(
         for r in range(3):
             nc.tensor.matmul_mx(
                 out=warm_bank[:],
-                lhsT=word_table[:, 0 : P // 2].bitcast(FP4X4),
-                lhsT_scale=w_planes[:, 1, :].bitcast(U8)[:, 0:P],
+                lhsT=w_sb[:, 1, 0 : 2 * P].bitcast(FP4X4),
+                lhsT_scale=late_scales[:, min(r, 1) * J : min(r, 1) * J + P],
                 rhs=w_sb[:, 0, :].bitcast(FP4X4),
                 rhs_scale=w_planes[:, 0, :].bitcast(U8),
                 start=True,

@@ -23,6 +23,8 @@ JT = J // P
 NT = N // P
 LIST_COLS = J // 16
 PAIR = 2 * J
+JOINED = (0, 2, 3)
+BY_VECTOR = (1,)
 
 
 def tile_list_interp_silu_kernel(
@@ -104,11 +106,11 @@ def tile_list_interp_silu_kernel(
         nc.sync.dma_start(x_raw[:], x.rearrange("(p i) j -> p i j", i=4))
         late_scales = move_scales(1)
         load_column(nc.sync, 2, iw2)
-        load_column(nc.sync, 3, iw3)
         wx_sb = sb("wx_sb", [P, 2 * N], U8)
         nc.sync.dma_start(wx_sb[:].bitcast(I32), wx_words[0].bitcast(I32))
         for q in range(4):
             nc.sync.dma_start(wx_plane[32 * q : 32 * q + 4, :], wx_scales.bitcast(I32)[0, 4 * q : 4 * q + 4, :])
+        load_column(nc.sync, 3, iw3)
         load_column(nc.sync, 4, b)
 
         parted = {}
@@ -167,18 +169,23 @@ def tile_list_interp_silu_kernel(
         def neighbour(g):
             for jt in range(JT):
                 bank = project(g, jt)
+                if (g, jt) == (G - 1, JT - 1):
+                    return bank
                 part = sb(f"part{g}_{jt}", [P, N], F32)
                 weight = columns[g][:, jt : jt + 1]
                 if g < 2:
                     nc.scalar.activation(part[:], bank[:], ACT.Copy, scale=weight)
                 else:
                     nc.vector.scalar_tensor_tensor(part[:], bank[:], weight, parts[g - 1, jt][:], ALU.mult, ALU.add)
+                if g == 2 and jt in JOINED:
+                    joined = sb(f"joined{jt}", [P, N], F32)
+                    nc.gpsimd.tensor_tensor(joined[:], part[:], parts[0, jt][:], ALU.add)
+                    part = joined
                 parts[g, jt] = part
 
-        for g in range(G - 1):
-            neighbour(g)
+        neighbour(0)
 
-        x_codes = sb("x_codes", [P, J], U32, tag=f"part1_{JT - 2}")
+        x_codes = sb("x_codes", [P, J], U32)
         x_plane = sb("x_plane", [P, J], U8)
         for jp in range(2):
             cols = slice(2 * jp * P, 2 * (jp + 1) * P)
@@ -187,7 +194,8 @@ def tile_list_interp_silu_kernel(
             nc.vector.quantize_mx(
                 out=x_codes[:, cols].bitcast(FP8X4), scales=x_plane[:, cols], in_=x_bf[:].rearrange("p j i -> p (j i)")
             )
-        neighbour(G - 1)
+        for g in range(1, G):
+            last_bank = neighbour(g)
 
         final = [
             [psum.tile([P, 2, 2 * P], F32, name=f"final{jp}_{half}", tag=f"bank{JT + 2 * jp + half}") for half in range(2)]
@@ -223,24 +231,33 @@ def tile_list_interp_silu_kernel(
             )
             skips[jt] = bank
             total[jt] = sb(f"total{jt}", [P, N], F32)
-            if jt < 2:
+            if jt not in BY_VECTOR:
                 nc.scalar.copy(total[jt][:], bank[:])
+
+        for jt in BY_VECTOR:
+            for half in range(2):
+                chans = slice(half * N // 2, (half + 1) * N // 2)
+                nc.vector.tensor_tensor(total[jt][:, chans], skips[jt][:, chans], parts[G - 1, jt][:, chans], ALU.add)
+        parts[G - 1, JT - 1] = sb("part_last", [P, N], F32)
+        nc.vector.scalar_tensor_tensor(
+            parts[G - 1, JT - 1][:], last_bank[:], columns[G - 1][:, JT - 1 : JT], parts[G - 2, JT - 1][:], ALU.mult, ALU.add
+        )
 
         out_view = out.rearrange("(t p) j -> p t j", p=P)
         for jp in range(2):
             for half in range(2):
-                chans = slice(half * N // 2, (half + 1) * N // 2)
-                for u in range(2):
-                    add_transposed(2 * jp + u, half, parts[0, 2 * jp + u], u == 0, False)
+                terms = []
                 for jt in (2 * jp, 2 * jp + 1):
-                    if jp == 0:
-                        add_transposed(jt, half, parts[G - 1, jt], False, False)
+                    if jt not in JOINED:
+                        terms = [(jt, parts[0, jt])] + terms
+                    if jt in BY_VECTOR:
+                        terms = terms + [(jt, total[jt])]
+                    elif jt < JT - 1:
+                        terms = terms + [(jt, parts[G - 1, jt]), (jt, total[jt])]
                     else:
-                        nc.vector.tensor_tensor(
-                            total[jt][:, chans], skips[jt][:, chans], parts[G - 1, jt][:, chans], ALU.add
-                        )
-                add_transposed(2 * jp, half, total[2 * jp], False, False)
-                add_transposed(2 * jp + 1, half, total[2 * jp + 1], False, True)
+                        terms = [(jt, total[jt])] + terms + [(jt, parts[G - 1, jt])]
+                for k, (jt, term) in enumerate(terms):
+                    add_transposed(jt, half, term, k == 0, k == len(terms) - 1)
                 for v in range(2):
                     nt = 2 * half + v
                     result = sb(f"result{jp}_{nt}", [P, 2 * P], F32)

@@ -24,7 +24,7 @@ NT = N // P
 LIST_COLS = J // 16
 PAIR = 2 * J
 JOINED = (0, 2, 3)
-BY_VECTOR = (1,)
+BY_VECTOR = (2,)
 
 
 def tile_list_interp_silu_kernel(
@@ -52,13 +52,13 @@ def tile_list_interp_silu_kernel(
         for a in range(2):
             nc.vector.memset(tab_planes[0][a][:], 0)
         for a in range(2):
-            nc.gpsimd.memset(tab_planes[1][a][:], 0)
+            nc.vector.memset(tab_planes[1][a][:], 0)
         wx_plane = sb("wx_plane", [P, N // 4], I32)
-        nc.gpsimd.memset(wx_plane[:], 0)
+        nc.vector.memset(wx_plane[:], 0)
 
         w_sb = sb("w_sb", [P, 2, 2 * N], U8)
         nc.sync.dma_start(w_sb[:].bitcast(I32), w_words.bitcast(I32).rearrange("a p n -> p a n"))
-        for q in range(4):
+        for q in (0, 2, 1, 3):
             nc.sync.dma_start(
                 w_planes[32 * q : 32 * q + 4, :, :],
                 w_scales.bitcast(I32)[:, 4 * q : 4 * q + 4, :].rearrange("a r n -> r a n"),
@@ -66,7 +66,7 @@ def tile_list_interp_silu_kernel(
         word_table = sb("word_table", [P, T], I32)
         nc.sync.dma_start(word_table[:], tab_words[0].rearrange("p t c -> p (t c)").bitcast(I32))
 
-        columns = {slot: sb(f"column{slot}", [P, JT], F32)[:] for slot in range(2, G + 1)}
+        columns = {slot: sb(f"column{slot}", [P, JT], F32)[:] for slot in range(G, G + 1)}
 
         def load_column(queue, slot, vec):
             with nc.allow_non_contiguous_dma(reason="one value a partition"):
@@ -77,13 +77,13 @@ def tile_list_interp_silu_kernel(
         make_identity(nc, ident[:])
         rows = sb("rows", [P, P], F32)
         nc.gpsimd.memset(rows[:], 0.0)
-        for slot, vec in enumerate((iw0, iw1)):
+        for slot, vec in enumerate((iw0, iw1, iw2, iw3)):
             nc.gpsimd.dma_start(rows[JT * slot : JT * (slot + 1), :], vec.rearrange("(t p) -> t p", p=P))
         turned = psum.tile([P, P], F32, name="turned", tag=f"bank{2 * JT - 2}")
         nc.tensor.matmul(turned[:], lhsT=rows[:], rhs=ident[:], is_transpose=True, start=True, stop=True)
-        early = sb("early", [P, 2 * JT], F32)
-        nc.scalar.copy(early[:], turned[:, 0 : 2 * JT])
-        for slot in range(2):
+        early = sb("early", [P, G * JT], F32)
+        nc.scalar.copy(early[:], turned[:, 0 : G * JT])
+        for slot in range(G):
             columns[slot] = early[:, JT * slot : JT * (slot + 1)]
 
         def move_scales(h):
@@ -105,12 +105,10 @@ def tile_list_interp_silu_kernel(
         x_raw = sb("x_raw", [P, 4, J], F32)
         nc.sync.dma_start(x_raw[:], x.rearrange("(p i) j -> p i j", i=4))
         late_scales = move_scales(1)
-        load_column(nc.sync, 2, iw2)
         wx_sb = sb("wx_sb", [P, 2 * N], U8)
         nc.sync.dma_start(wx_sb[:].bitcast(I32), wx_words[0].bitcast(I32))
         for q in range(4):
             nc.sync.dma_start(wx_plane[32 * q : 32 * q + 4, :], wx_scales.bitcast(I32)[0, 4 * q : 4 * q + 4, :])
-        load_column(nc.sync, 3, iw3)
         load_column(nc.sync, 4, b)
 
         parted = {}
@@ -190,17 +188,14 @@ def tile_list_interp_silu_kernel(
         for jp in range(2):
             cols = slice(2 * jp * P, 2 * (jp + 1) * P)
             x_bf = sb(f"x_bf{jp}", [P, 2 * P, 4], BF16)
-            nc.scalar.copy(x_bf[:], x_raw[:, :, cols].rearrange("p i j -> p j i"))
+            nc.scalar.copy(
+                x_bf[:].rearrange("p (c j) i -> p c i j", j=4), x_raw[:, :, cols].rearrange("p i (c j) -> p c i j", j=4)
+            )
             nc.vector.quantize_mx(
                 out=x_codes[:, cols].bitcast(FP8X4), scales=x_plane[:, cols], in_=x_bf[:].rearrange("p j i -> p (j i)")
             )
         for g in range(1, G):
             last_bank = neighbour(g)
-
-        final = [
-            [psum.tile([P, 2, 2 * P], F32, name=f"final{jp}_{half}", tag=f"bank{JT + 2 * jp + half}") for half in range(2)]
-            for jp in range(2)
-        ]
 
         def add_transposed(jt, half, part, first, last):
             jp, u = divmod(jt, 2)
@@ -238,28 +233,41 @@ def tile_list_interp_silu_kernel(
             for half in range(2):
                 chans = slice(half * N // 2, (half + 1) * N // 2)
                 nc.vector.tensor_tensor(total[jt][:, chans], skips[jt][:, chans], parts[G - 1, jt][:, chans], ALU.add)
-        parts[G - 1, JT - 1] = sb("part_last", [P, N], F32)
-        nc.vector.scalar_tensor_tensor(
-            parts[G - 1, JT - 1][:], last_bank[:], columns[G - 1][:, JT - 1 : JT], parts[G - 2, JT - 1][:], ALU.mult, ALU.add
-        )
+        last = parts[G - 1, JT - 2]
+        for half in range(2):
+            chans = slice(half * N // 2, (half + 1) * N // 2)
+            nc.vector.scalar_tensor_tensor(
+                last[:, chans],
+                last_bank[:, chans],
+                columns[G - 1][:, JT - 1 : JT],
+                parts[G - 2, JT - 1][:, chans],
+                ALU.mult,
+                ALU.add,
+            )
+
+        final = [
+            [psum.tile([P, 2, 2 * P], F32, name=f"final{jp}_{half}", tag=f"bank{JT * (1 - jp) + half}") for half in range(2)]
+            for jp in range(2)
+        ]
 
         out_view = out.rearrange("(t p) j -> p t j", p=P)
-        for jp in range(2):
-            for half in range(2):
-                terms = []
-                for jt in (2 * jp, 2 * jp + 1):
-                    if jt not in JOINED:
-                        terms = [(jt, parts[0, jt])] + terms
-                    if jt in BY_VECTOR:
-                        terms = terms + [(jt, total[jt])]
-                    elif jt < JT - 1:
-                        terms = terms + [(jt, parts[G - 1, jt]), (jt, total[jt])]
-                    else:
-                        terms = [(jt, total[jt])] + terms + [(jt, parts[G - 1, jt])]
-                for k, (jt, term) in enumerate(terms):
-                    add_transposed(jt, half, term, k == 0, k == len(terms) - 1)
-                for v in range(2):
-                    nt = 2 * half + v
-                    result = sb(f"result{jp}_{nt}", [P, 2 * P], F32)
-                    nc.scalar.activation(result[:], final[jp][half][:, v, :], ACT.Silu, bias=columns[G][:, nt : nt + 1])
-                    nc.sync.dma_start(out_view[:, nt, 2 * jp * P : 2 * (jp + 1) * P], result[:])
+
+        def finish(jp, half):
+            for v in range(2):
+                nt = 2 * half + v
+                result = sb(f"result{jp}_{nt}", [P, 2 * P], F32)
+                nc.scalar.activation(result[:], final[jp][half][:, v, :], ACT.Silu, bias=columns[G][:, nt : nt + 1])
+                nc.sync.dma_start(out_view[:, nt, 2 * jp * P : 2 * (jp + 1) * P], result[:])
+
+        for half in range(2):
+            add_transposed(1, half, parts[0, 1], True, False)
+            add_transposed(0, half, parts[G - 1, 0], False, False)
+            add_transposed(0, half, total[0], False, False)
+            add_transposed(1, half, parts[G - 1, 1], False, False)
+            add_transposed(1, half, total[1], False, True)
+            finish(0, half)
+        for half in range(2):
+            add_transposed(3, half, total[3], True, False)
+            add_transposed(2, half, total[2], False, False)
+            add_transposed(3, half, last, False, True)
+            finish(1, half)

@@ -24,7 +24,7 @@ NT = N // P
 LIST_COLS = J // 16
 PAIR = 2 * J
 JOINED = (0, 2, 3)
-BY_VECTOR = (2,)
+FINAL_BANKS = ((0, 1, 4, 5), (6, 3, 0, 1))
 
 
 def tile_list_interp_silu_kernel(
@@ -164,24 +164,22 @@ def tile_list_interp_silu_kernel(
 
         parts = {}
 
-        def neighbour(g):
-            for jt in range(JT):
-                bank = project(g, jt)
-                if (g, jt) == (G - 1, JT - 1):
-                    return bank
-                part = sb(f"part{g}_{jt}", [P, N], F32)
-                weight = columns[g][:, jt : jt + 1]
-                if g < 2:
-                    nc.scalar.activation(part[:], bank[:], ACT.Copy, scale=weight)
-                else:
-                    nc.vector.scalar_tensor_tensor(part[:], bank[:], weight, parts[g - 1, jt][:], ALU.mult, ALU.add)
-                if g == 2 and jt in JOINED:
-                    joined = sb(f"joined{jt}", [P, N], F32)
-                    nc.gpsimd.tensor_tensor(joined[:], part[:], parts[0, jt][:], ALU.add)
-                    part = joined
-                parts[g, jt] = part
+        def neighbour(g, jt):
+            bank = project(g, jt)
+            part = sb(f"part{g}_{jt}", [P, N], F32)
+            weight = columns[g][:, jt : jt + 1]
+            if g < 2:
+                nc.scalar.activation(part[:], bank[:], ACT.Copy, scale=weight)
+            else:
+                nc.vector.scalar_tensor_tensor(part[:], bank[:], weight, parts[g - 1, jt][:], ALU.mult, ALU.add)
+            if g == 2 and jt in JOINED:
+                joined = sb(f"joined{jt}", [P, N], F32)
+                nc.gpsimd.tensor_tensor(joined[:], part[:], parts[0, jt][:], ALU.add)
+                part = joined
+            parts[g, jt] = part
 
-        neighbour(0)
+        for jt in range(JT):
+            neighbour(0, jt)
 
         x_codes = sb("x_codes", [P, J], U32)
         x_plane = sb("x_plane", [P, J], U8)
@@ -194,25 +192,11 @@ def tile_list_interp_silu_kernel(
             nc.vector.quantize_mx(
                 out=x_codes[:, cols].bitcast(FP8X4), scales=x_plane[:, cols], in_=x_bf[:].rearrange("p j i -> p (j i)")
             )
-        for g in range(1, G):
-            last_bank = neighbour(g)
+        for g in (1, 2):
+            for jt in range(JT):
+                neighbour(g, jt)
 
-        def add_transposed(jt, half, part, first, last):
-            jp, u = divmod(jt, 2)
-            for v in range(2):
-                nt = 2 * half + v
-                nc.tensor.matmul(
-                    final[jp][half][:, v, u * P : (u + 1) * P],
-                    lhsT=part[:, nt * P : (nt + 1) * P],
-                    rhs=ident[:],
-                    is_transpose=True,
-                    start=(first and v == 0),
-                    stop=(last and v == 1),
-                )
-
-        total = {}
-        skips = {}
-        for jt in range(JT):
+        def skip_product(jt):
             cols = slice(jt * P, (jt + 1) * P)
             bank = psum.tile([P, N], F32, name=f"skip{jt}", tag=f"bank{jt}")
             nc.tensor.matmul_mx(
@@ -224,50 +208,49 @@ def tile_list_interp_silu_kernel(
                 start=True,
                 stop=True,
             )
-            skips[jt] = bank
-            total[jt] = sb(f"total{jt}", [P, N], F32)
-            if jt not in BY_VECTOR:
-                nc.scalar.copy(total[jt][:], bank[:])
+            return bank
 
-        for jt in BY_VECTOR:
-            for half in range(2):
-                chans = slice(half * N // 2, (half + 1) * N // 2)
-                nc.vector.tensor_tensor(total[jt][:, chans], skips[jt][:, chans], parts[G - 1, jt][:, chans], ALU.add)
-        last = parts[G - 1, JT - 2]
-        for half in range(2):
-            chans = slice(half * N // 2, (half + 1) * N // 2)
+        def skip_term(jt):
+            term = sb(f"skip_term{jt}", [P, N], F32)
+            nc.scalar.copy(term[:], skip_product(jt)[:])
+            return term
+
+        neighbour(3, 0)
+        neighbour(3, 1)
+        neighbour(3, 2)
+        skip0 = skip_term(0)
+        skip1 = skip_term(1)
+        last_bank = project(3, 3)
+        skip3 = skip_term(3)
+        skip_bank2 = skip_product(2)
+
+        total2 = sb("total2", [P, N], F32)
+        halves = [slice(half * N // 2, (half + 1) * N // 2) for half in range(2)]
+        for chans in halves:
+            nc.vector.tensor_tensor(total2[:, chans], skip_bank2[:, chans], parts[3, 2][:, chans], ALU.add)
+        last = parts[3, 2]
+        for chans in halves:
             nc.vector.scalar_tensor_tensor(
-                last[:, chans],
-                last_bank[:, chans],
-                columns[G - 1][:, JT - 1 : JT],
-                parts[G - 2, JT - 1][:, chans],
-                ALU.mult,
-                ALU.add,
+                last[:, chans], last_bank[:, chans], columns[3][:, 3:4], parts[2, 3][:, chans], ALU.mult, ALU.add
             )
 
-        final = [
-            [psum.tile([P, 2, 2 * P], F32, name=f"final{jp}_{half}", tag=f"bank{JT * (1 - jp) + half}") for half in range(2)]
-            for jp in range(2)
-        ]
-
         out_view = out.rearrange("(t p) j -> p t j", p=P)
-
-        def finish(jp, half):
-            for v in range(2):
-                nt = 2 * half + v
+        terms = (
+            ((1, parts[0, 1]), (0, skip0), (1, skip1), (0, parts[3, 0]), (1, parts[3, 1])),
+            ((1, skip3), (0, total2), (1, last)),
+        )
+        for jp in range(2):
+            for nt in range(NT):
+                final = psum.tile([P, 2 * P], F32, name=f"final{jp}_{nt}", tag=f"bank{FINAL_BANKS[jp][nt]}")
+                for k, (u, term) in enumerate(terms[jp]):
+                    nc.tensor.matmul(
+                        final[:, u * P : (u + 1) * P],
+                        lhsT=term[:, nt * P : (nt + 1) * P],
+                        rhs=ident[:],
+                        is_transpose=True,
+                        start=(k == 0),
+                        stop=(k == len(terms[jp]) - 1),
+                    )
                 result = sb(f"result{jp}_{nt}", [P, 2 * P], F32)
-                nc.scalar.activation(result[:], final[jp][half][:, v, :], ACT.Silu, bias=columns[G][:, nt : nt + 1])
+                nc.scalar.activation(result[:], final[:], ACT.Silu, bias=columns[G][:, nt : nt + 1])
                 nc.sync.dma_start(out_view[:, nt, 2 * jp * P : 2 * (jp + 1) * P], result[:])
-
-        for half in range(2):
-            add_transposed(1, half, parts[0, 1], True, False)
-            add_transposed(0, half, parts[G - 1, 0], False, False)
-            add_transposed(0, half, total[0], False, False)
-            add_transposed(1, half, parts[G - 1, 1], False, False)
-            add_transposed(1, half, total[1], False, True)
-            finish(0, half)
-        for half in range(2):
-            add_transposed(3, half, total[3], True, False)
-            add_transposed(2, half, total[2], False, False)
-            add_transposed(3, half, last, False, True)
-            finish(1, half)

@@ -43,7 +43,11 @@ def tile_list_interp_silu_kernel(
         nc.sync.dma_start(scale_table[96:P, :], tab_scales.bitcast(I32).rearrange("a q t -> (a q) t"))
         nc.sync.dma_start(offsets[:], offs)
         w_planes = sb("w_planes", [P, 2, N // 4], I32)
-        nc.gpsimd.memset(w_planes[:], 0)
+        nc.vector.memset(w_planes[:], 0)
+        rows = sb("rows", [P, P], F32)
+        nc.gpsimd.memset(rows[:], 0.0)
+        for slot, vec in enumerate((iw0, iw1, iw2, iw3)):
+            nc.gpsimd.dma_start(rows[JT * slot : JT * (slot + 1), :], vec.rearrange("(t p) -> t p", p=P))
         nc.vector.memset(scale_table[0:96, :], 0)
         warm = sb("warm", [P, 16], F32)
         nc.vector.memset(warm[:, 0:1], 0.0)
@@ -75,10 +79,6 @@ def tile_list_interp_silu_kernel(
 
         ident = sb("ident", [P, P], F32)
         make_identity(nc, ident[:])
-        rows = sb("rows", [P, P], F32)
-        nc.gpsimd.memset(rows[:], 0.0)
-        for slot, vec in enumerate((iw0, iw1, iw2, iw3)):
-            nc.gpsimd.dma_start(rows[JT * slot : JT * (slot + 1), :], vec.rearrange("(t p) -> t p", p=P))
         turned = psum.tile([P, P], F32, name="turned", tag=f"bank{2 * JT - 2}")
         nc.tensor.matmul(turned[:], lhsT=rows[:], rhs=ident[:], is_transpose=True, start=True, stop=True)
         early = sb("early", [P, G * JT], F32)
@@ -97,8 +97,7 @@ def tile_list_interp_silu_kernel(
             order = [(q, a) for q in (0, 2, 1, 3) for a in (1, 0)]
             for q, a in order:
                 row = 96 + 16 * a + 4 * q
-                queue = nc.gpsimd if (h, q, a) == (1, 0, 1) else nc.sync
-                queue.dma_start(tab_planes[h][a][32 * q : 32 * q + 4, :], picked_scales[row : row + 4, :].bitcast(I32))
+                nc.sync.dma_start(tab_planes[h][a][32 * q : 32 * q + 4, :], picked_scales[row : row + 4, :].bitcast(I32))
             return picked_scales
 
         move_scales(0)

@@ -46,19 +46,17 @@ def tile_list_interp_silu_kernel(
         nc.vector.memset(w_planes[:], 0)
         rows = sb("rows", [P, P], F32)
         nc.gpsimd.memset(rows[:], 0.0)
-        for slot, vec in enumerate((iw0, iw1, iw2, iw3)):
+        ident = sb("ident", [P, P], F32)
+        make_identity(nc, ident[:])
+        for slot, vec in enumerate((iw0, iw1, iw2)):
             nc.gpsimd.dma_start(rows[JT * slot : JT * (slot + 1), :], vec.rearrange("(t p) -> t p", p=P))
         nc.vector.memset(scale_table[0:96, :], 0)
         warm = sb("warm", [P, 16], F32)
         nc.vector.memset(warm[:, 0:1], 0.0)
         nc.scalar.activation(warm[:, 8:9], warm[:, 0:1], ACT.Silu)
-        tab_planes = [[sb(f"tab_plane{h}_{a}", [P, PAIR // 4], I32) for a in range(2)] for h in range(2)]
-        for a in range(2):
-            nc.vector.memset(tab_planes[0][a][:], 0)
-        for a in range(2):
-            nc.vector.memset(tab_planes[1][a][:], 0)
-        wx_plane = sb("wx_plane", [P, N // 4], I32)
-        nc.vector.memset(wx_plane[:], 0)
+        first_planes = sb("first_planes", [P, 2, PAIR // 4], I32)
+        nc.vector.memset(first_planes[:], 0)
+        tab_planes = [[first_planes[:, a, :] for a in range(2)]]
 
         w_sb = sb("w_sb", [P, 2, 2 * N], U8)
         nc.sync.dma_start(w_sb[:].bitcast(I32), w_words.bitcast(I32).rearrange("a p n -> p a n"))
@@ -70,20 +68,17 @@ def tile_list_interp_silu_kernel(
         word_table = sb("word_table", [P, T], I32)
         nc.sync.dma_start(word_table[:], tab_words[0].rearrange("p t c -> p (t c)").bitcast(I32))
 
-        columns = {slot: sb(f"column{slot}", [P, JT], F32)[:] for slot in range(G, G + 1)}
+        columns = {slot: sb(f"column{slot}", [P, JT], F32)[:] for slot in range(G - 1, G + 1)}
 
         def load_column(queue, slot, vec):
             with nc.allow_non_contiguous_dma(reason="one value a partition"):
                 queue.dma_start(columns[slot], vec.rearrange("(t p) -> p t", p=P))
 
-
-        ident = sb("ident", [P, P], F32)
-        make_identity(nc, ident[:])
         turned = psum.tile([P, P], F32, name="turned", tag=f"bank{2 * JT - 2}")
         nc.tensor.matmul(turned[:], lhsT=rows[:], rhs=ident[:], is_transpose=True, start=True, stop=True)
-        early = sb("early", [P, G * JT], F32)
-        nc.scalar.copy(early[:], turned[:, 0 : G * JT])
-        for slot in range(G):
+        early = sb("early", [P, (G - 1) * JT], F32)
+        nc.scalar.copy(early[:], turned[:, 0 : (G - 1) * JT])
+        for slot in range(G - 1):
             columns[slot] = early[:, JT * slot : JT * (slot + 1)]
 
         def move_scales(h):
@@ -94,6 +89,9 @@ def tile_list_interp_silu_kernel(
                     picked_scales[:, u * J : (u + 1) * J],
                     scale_table[:].bitcast(U8).indirect(offsets[:, g * LIST_COLS : (g + 1) * LIST_COLS]),
                 )
+            if h == 1:
+                second_planes = sb("second_planes", [P, 2, PAIR // 4], I32, tag="scale_table")
+                tab_planes.append([second_planes[:, a, :] for a in range(2)])
             order = [(q, a) for q in (0, 2, 1, 3) for a in (1, 0)]
             for q, a in order:
                 row = 96 + 16 * a + 4 * q
@@ -106,7 +104,10 @@ def tile_list_interp_silu_kernel(
         late_scales = move_scales(1)
         wx_sb = sb("wx_sb", [P, 2 * N], U8)
         nc.sync.dma_start(wx_sb[:].bitcast(I32), wx_words[0].bitcast(I32))
+        wx_plane = sb("wx_plane", [P, N // 4], I32, tag="picked_scales0")
         for q in range(4):
+            if q == 2:
+                load_column(nc.sync, 3, iw3)
             nc.sync.dma_start(wx_plane[32 * q : 32 * q + 4, :], wx_scales.bitcast(I32)[0, 4 * q : 4 * q + 4, :])
         load_column(nc.sync, 4, b)
 
@@ -170,10 +171,10 @@ def tile_list_interp_silu_kernel(
             if g < 2:
                 nc.scalar.activation(part[:], bank[:], ACT.Copy, scale=weight)
             else:
-                nc.vector.scalar_tensor_tensor(part[:], bank[:], weight, parts[g - 1, jt][:], ALU.mult, ALU.add)
+                nc.vector.scalar_tensor_tensor(part[:], bank[:], weight, parts[2 * (g - 2), jt][:], ALU.mult, ALU.add)
             if g == 2 and jt in JOINED:
                 joined = sb(f"joined{jt}", [P, N], F32)
-                nc.gpsimd.tensor_tensor(joined[:], part[:], parts[0, jt][:], ALU.add)
+                nc.gpsimd.tensor_tensor(joined[:], part[:], parts[1, jt][:], ALU.add)
                 part = joined
             parts[g, jt] = part
 
@@ -235,7 +236,7 @@ def tile_list_interp_silu_kernel(
 
         out_view = out.rearrange("(t p) j -> p t j", p=P)
         terms = (
-            ((1, parts[0, 1]), (0, skip0), (1, skip1), (0, parts[3, 0]), (1, parts[3, 1])),
+            ((1, parts[1, 1]), (0, skip0), (1, skip1), (0, parts[3, 0]), (1, parts[3, 1])),
             ((1, skip3), (0, total2), (1, last)),
         )
         for jp in range(2):

@@ -24,7 +24,7 @@ NT = N // P
 LIST_COLS = J // 16
 PAIR = 2 * J
 JOINED = (0, 2, 3)
-FINAL_BANKS = ((0, 1, 4, 5), (6, 3, 0, 1))
+FINAL_BANKS = ((0, 4, 5, 1), (3, 6, 0, 4))
 
 
 def tile_list_interp_silu_kernel(
@@ -217,26 +217,35 @@ def tile_list_interp_silu_kernel(
 
         neighbour(3, 0)
         neighbour(3, 1)
-        neighbour(3, 2)
+        third_bank = project(3, 2)
         skip0 = skip_term(0)
-        skip1 = skip_term(1)
-        last_bank = project(3, 3)
-        skip3 = skip_term(3)
-        skip_bank2 = skip_product(2)
-
-        total2 = sb("total2", [P, N], F32)
+        skip1 = sb("skip_term1", [P, N], F32)
+        skip_bank1 = skip_product(1)
         halves = [slice(half * N // 2, (half + 1) * N // 2) for half in range(2)]
         for chans in halves:
-            nc.vector.tensor_tensor(total2[:, chans], skip_bank2[:, chans], parts[3, 2][:, chans], ALU.add)
-        last = parts[3, 2]
-        for chans in halves:
+            nc.vector.tensor_tensor(skip1[:, chans], skip_bank1[:, chans], parts[1, 1][:, chans], ALU.add)
+        skip_bank2 = skip_product(2)
+        last_bank = project(3, 3)
+        skip3 = skip_term(3)
+
+        third = parts[1, 1]
+        last = parts[2, 2]
+
+        def add_last_neighbour(total, bank, jt, chans):
             nc.vector.scalar_tensor_tensor(
-                last[:, chans], last_bank[:, chans], columns[3][:, 3:4], parts[2, 3][:, chans], ALU.mult, ALU.add
+                total[:, chans], bank[:, chans], columns[3][:, jt : jt + 1], parts[2, jt][:, chans], ALU.mult, ALU.add
             )
+
+        for chans in halves:
+            add_last_neighbour(third, third_bank, 2, chans)
+        total2 = sb("total2", [P, N], F32)
+        for chans in halves:
+            nc.vector.tensor_tensor(total2[:, chans], skip_bank2[:, chans], third[:, chans], ALU.add)
+            add_last_neighbour(last, last_bank, 3, chans)
 
         out_view = out.rearrange("(t p) j -> p t j", p=P)
         terms = (
-            ((1, parts[1, 1]), (0, skip0), (1, skip1), (0, parts[3, 0]), (1, parts[3, 1])),
+            ((0, parts[3, 0]), (0, skip0), (1, parts[3, 1]), (1, skip1)),
             ((1, skip3), (0, total2), (1, last)),
         )
         for jp in range(2):

@@ -53,7 +53,6 @@ def tile_list_interp_silu_kernel(
         nc.vector.memset(scale_table[0:96, :], 0)
         warm = sb("warm", [P, 16], F32)
         nc.vector.memset(warm[:, 0:1], 0.0)
-        nc.scalar.activation(warm[:, 8:9], warm[:, 0:1], ACT.Silu)
         first_planes = sb("first_planes", [P, 2, PAIR // 4], I32)
         nc.vector.memset(first_planes[:], 0)
         tab_planes = [[first_planes[:, a, :] for a in range(2)]]
@@ -61,10 +60,11 @@ def tile_list_interp_silu_kernel(
         w_sb = sb("w_sb", [P, 2, 2 * N], U8)
         nc.sync.dma_start(w_sb[:].bitcast(I32), w_words.bitcast(I32).rearrange("a p n -> p a n"))
         for q in (0, 2, 1, 3):
-            nc.sync.dma_start(
+            nc.scalar.dma_start(
                 w_planes[32 * q : 32 * q + 4, :, :],
                 w_scales.bitcast(I32)[:, 4 * q : 4 * q + 4, :].rearrange("a r n -> r a n"),
             )
+        nc.scalar.activation(warm[:, 8:9], warm[:, 0:1], ACT.Silu)
         word_table = sb("word_table", [P, T], I32)
         nc.sync.dma_start(word_table[:], tab_words[0].rearrange("p t c -> p (t c)").bitcast(I32))
 

@@ -23,8 +23,7 @@ JT = J // P
 NT = N // P
 LIST_COLS = J // 16
 PAIR = 2 * J
-JOINED = (0, 2, 3)
-FINAL_BANKS = ((0, 4, 5, 1), (3, 6, 0, 4))
+FINAL_BANKS = {1: (4, 5, 6, 7), 0: (2, 3, 4, 5)}
 
 
 def tile_list_interp_silu_kernel(
@@ -106,9 +105,8 @@ def tile_list_interp_silu_kernel(
         nc.sync.dma_start(wx_sb[:].bitcast(I32), wx_words[0].bitcast(I32))
         wx_plane = sb("wx_plane", [P, N // 4], I32, tag="picked_scales0")
         for q in range(4):
-            if q == 2:
-                load_column(nc.sync, 3, iw3)
             nc.sync.dma_start(wx_plane[32 * q : 32 * q + 4, :], wx_scales.bitcast(I32)[0, 4 * q : 4 * q + 4, :])
+        load_column(nc.sync, 3, iw3)
         load_column(nc.sync, 4, b)
 
         parted = {}
@@ -124,16 +122,27 @@ def tile_list_interp_silu_kernel(
                 picked[:, base + j0 : base + j1].bitcast(U16).rearrange("p (j d) -> p d j", d=2),
             )
 
-        for g in range(G):
+        def gather_words(g):
             base = (G - 1 - g) * (J - P)
             nc.vector.tensor_copy(
                 picked[:, base : base + J],
                 word_table[:].bitcast(U32).indirect(offsets[:, g * LIST_COLS : (g + 1) * LIST_COLS]),
             )
+
+        for g in range(2):
+            gather_words(g)
             if g > 0:
                 part_words(g - 1, J - P, J)
             part_words(g, 0, P)
-            part_words(g, P, J - P if g < G - 1 else J)
+            part_words(g, P, J - P)
+        gather_words(2)
+        part_words(1, J - P, J)
+        for jt in (0, 2, 3):
+            part_words(2, jt * P, (jt + 1) * P)
+        gather_words(3)
+        part_words(2, P, 2 * P)
+        part_words(3, 2 * P, J)
+        part_words(3, 0, 2 * P)
 
         warm_bank = psum.tile([P, N], F32, name="warm_bank", tag=f"bank{2 * JT - 1}")
         for r in range(3):
@@ -147,8 +156,8 @@ def tile_list_interp_silu_kernel(
                 stop=True,
             )
 
-        def project(g, jt):
-            bank = psum.tile([P, N], F32, name=f"acc{g}_{jt}", tag=f"bank{JT * (g % 2) + jt}")
+        def project(g, jt, index):
+            bank = psum.tile([P, N], F32, name=f"acc{g}_{jt}", tag=f"bank{index}")
             c0 = g * J + jt * P
             for a in range(2):
                 nc.tensor.matmul_mx(
@@ -162,24 +171,38 @@ def tile_list_interp_silu_kernel(
                 )
             return bank
 
-        parts = {}
+        def channel_pieces(count):
+            return [slice(k * N // count, (k + 1) * N // count) for k in range(count)]
 
-        def neighbour(g, jt):
-            bank = project(g, jt)
-            part = sb(f"part{g}_{jt}", [P, N], F32)
-            weight = columns[g][:, jt : jt + 1]
-            if g < 2:
-                nc.scalar.activation(part[:], bank[:], ACT.Copy, scale=weight)
-            else:
-                nc.vector.scalar_tensor_tensor(part[:], bank[:], weight, parts[2 * (g - 2), jt][:], ALU.mult, ALU.add)
-            if g == 2 and jt in JOINED:
-                joined = sb(f"joined{jt}", [P, N], F32)
-                nc.gpsimd.tensor_tensor(joined[:], part[:], parts[1, jt][:], ALU.add)
-                part = joined
-            parts[g, jt] = part
+        term = {}
+
+        def scalar_term(g, jt, bank):
+            term[g, jt] = sb(f"term{g}_{jt}", [P, N], F32)
+            nc.scalar.activation(term[g, jt][:], bank[:], ACT.Copy, scale=columns[g][:, jt : jt + 1])
+
+        def add_weighted(total, g, jt, bank, other, chans):
+            nc.vector.scalar_tensor_tensor(
+                total[:, chans], bank[:, chans], columns[g][:, jt : jt + 1], other[:, chans], ALU.mult, ALU.add
+            )
+
+        def weighted_sum(g, jt, bank, other):
+            total = sb(f"sum{g}_{jt}", [P, N], F32)
+            add_weighted(total, g, jt, bank, other, slice(0, N))
+            return total
+
+        def skip_sum(jt, bank, other, count):
+            total = sb(f"skip_sum{jt}", [P, N], F32)
+            for chans in channel_pieces(count):
+                nc.vector.tensor_tensor(total[:, chans], bank[:, chans], other[:, chans], ALU.add)
+            return total
+
+        def join(name, first, second, tag=None):
+            joined = sb(name, [P, N], F32, tag=tag)
+            nc.gpsimd.tensor_tensor(joined[:], first[:], second[:], ALU.add)
+            return joined
 
         for jt in range(JT):
-            neighbour(0, jt)
+            scalar_term(0, jt, project(0, jt, jt))
 
         x_codes = sb("x_codes", [P, J], U32)
         x_plane = sb("x_plane", [P, J], U8)
@@ -192,13 +215,15 @@ def tile_list_interp_silu_kernel(
             nc.vector.quantize_mx(
                 out=x_codes[:, cols].bitcast(FP8X4), scales=x_plane[:, cols], in_=x_bf[:].rearrange("p j i -> p (j i)")
             )
-        for g in (1, 2):
-            for jt in range(JT):
-                neighbour(g, jt)
+        for jt in range(JT):
+            scalar_term(1, jt, project(1, jt, JT + jt))
+        acc2 = {jt: project(2, jt, jt) for jt in (2, 3, 0, 1)}
+        for jt in range(2):
+            scalar_term(2, jt, acc2[jt])
 
-        def skip_product(jt):
+        def skip_product(jt, index):
             cols = slice(jt * P, (jt + 1) * P)
-            bank = psum.tile([P, N], F32, name=f"skip{jt}", tag=f"bank{jt}")
+            bank = psum.tile([P, N], F32, name=f"skip{jt}", tag=f"bank{index}")
             nc.tensor.matmul_mx(
                 out=bank[:],
                 lhsT=x_codes[:, cols].bitcast(FP8X4),
@@ -210,55 +235,41 @@ def tile_list_interp_silu_kernel(
             )
             return bank
 
-        def skip_term(jt):
-            term = sb(f"skip_term{jt}", [P, N], F32)
-            nc.scalar.copy(term[:], skip_product(jt)[:])
-            return term
-
-        neighbour(3, 0)
-        neighbour(3, 1)
-        third_bank = project(3, 2)
-        skip0 = skip_term(0)
-        skip1 = sb("skip_term1", [P, N], F32)
-        skip_bank1 = skip_product(1)
-        halves = [slice(half * N // 2, (half + 1) * N // 2) for half in range(2)]
-        for chans in halves:
-            nc.vector.tensor_tensor(skip1[:, chans], skip_bank1[:, chans], parts[1, 1][:, chans], ALU.add)
-        skip_bank2 = skip_product(2)
-        last_bank = project(3, 3)
-        skip3 = skip_term(3)
-
-        third = parts[1, 1]
-        last = parts[2, 2]
-
-        def add_last_neighbour(total, bank, jt, chans):
-            nc.vector.scalar_tensor_tensor(
-                total[:, chans], bank[:, chans], columns[3][:, jt : jt + 1], parts[2, jt][:, chans], ALU.mult, ALU.add
-            )
-
-        for chans in halves:
-            add_last_neighbour(third, third_bank, 2, chans)
-        total2 = sb("total2", [P, N], F32)
-        for chans in halves:
-            nc.vector.tensor_tensor(total2[:, chans], skip_bank2[:, chans], third[:, chans], ALU.add)
-            add_last_neighbour(last, last_bank, 3, chans)
+        pair0 = join("pair0", term[0, 0], term[1, 0], tag="x_bf0")
+        pair1 = join("pair1", term[0, 1], term[1, 1], tag="x_bf1")
+        neighbours0 = join("neighbours0", pair0, term[2, 0])
+        sum22 = weighted_sum(2, 2, acc2[2], term[0, 2])
+        sum23 = weighted_sum(2, 3, acc2[3], term[0, 3])
+        sum32 = weighted_sum(3, 2, project(3, 2, 4), sum22)
+        sum33 = weighted_sum(3, 3, project(3, 3, 5), sum23)
+        skip_sum2 = skip_sum(2, skip_product(2, 6), sum32, 1)
+        skip_sum3 = skip_sum(3, skip_product(3, 7), sum33, 1)
+        sum31 = weighted_sum(3, 1, project(3, 1, 2), term[2, 1])
+        early0 = skip_sum(0, skip_product(0, 3), neighbours0, 2)
+        acc30 = project(3, 0, 0)
+        skip1 = skip_product(1, 1)
+        total0 = sb("total0", [P, N], F32)
+        skip_sum1 = sb("skip_sum1", [P, N], F32)
+        for chans in channel_pieces(NT):
+            nc.vector.tensor_tensor(skip_sum1[:, chans], skip1[:, chans], sum31[:, chans], ALU.add)
+            add_weighted(total0, 3, 0, acc30, early0, chans)
 
         out_view = out.rearrange("(t p) j -> p t j", p=P)
-        terms = (
-            ((0, parts[3, 0]), (0, skip0), (1, parts[3, 1]), (1, skip1)),
-            ((1, skip3), (0, total2), (1, last)),
-        )
-        for jp in range(2):
+        closing = {
+            1: ((1, skip_sum3), (0, skip_sum2), (0, term[1, 2]), (1, term[1, 3])),
+            0: ((1, pair1), (1, skip_sum1), (0, total0)),
+        }
+        for jp in (1, 0):
             for nt in range(NT):
                 final = psum.tile([P, 2 * P], F32, name=f"final{jp}_{nt}", tag=f"bank{FINAL_BANKS[jp][nt]}")
-                for k, (u, term) in enumerate(terms[jp]):
+                for k, (u, part) in enumerate(closing[jp]):
                     nc.tensor.matmul(
                         final[:, u * P : (u + 1) * P],
-                        lhsT=term[:, nt * P : (nt + 1) * P],
+                        lhsT=part[:, nt * P : (nt + 1) * P],
                         rhs=ident[:],
                         is_transpose=True,
                         start=(k == 0),
-                        stop=(k == len(terms[jp]) - 1),
+                        stop=(k == len(closing[jp]) - 1),
                     )
                 result = sb(f"result{jp}_{nt}", [P, 2 * P], F32)
                 nc.scalar.activation(result[:], final[:], ACT.Silu, bias=columns[G][:, nt : nt + 1])

@@ -23,7 +23,7 @@ JT = J // P
 NT = N // P
 LIST_COLS = J // 16
 PAIR = 2 * J
-FINAL_BANKS = {1: (4, 5, 6, 7), 0: (2, 3, 4, 5)}
+FINAL_BANKS = {1: (4, 5, 6, 7), 0: (2, 3, 1, 4)}
 
 
 def tile_list_interp_silu_kernel(
@@ -238,26 +238,26 @@ def tile_list_interp_silu_kernel(
         pair0 = join("pair0", term[0, 0], term[1, 0], tag="x_bf0")
         pair1 = join("pair1", term[0, 1], term[1, 1], tag="x_bf1")
         neighbours0 = join("neighbours0", pair0, term[2, 0])
+        neighbours1 = join("neighbours1", pair1, term[2, 1])
         sum22 = weighted_sum(2, 2, acc2[2], term[0, 2])
         sum23 = weighted_sum(2, 3, acc2[3], term[0, 3])
         sum32 = weighted_sum(3, 2, project(3, 2, 4), sum22)
         sum33 = weighted_sum(3, 3, project(3, 3, 5), sum23)
         skip_sum2 = skip_sum(2, skip_product(2, 6), sum32, 1)
         skip_sum3 = skip_sum(3, skip_product(3, 7), sum33, 1)
-        sum31 = weighted_sum(3, 1, project(3, 1, 2), term[2, 1])
-        early0 = skip_sum(0, skip_product(0, 3), neighbours0, 2)
+        skip_term1 = sb("skip_term1", [P, N], F32)
+        nc.scalar.copy(skip_term1[:], skip_product(1, 2)[:])
+        sum31 = weighted_sum(3, 1, project(3, 1, 3), skip_term1)
+        early0 = skip_sum(0, skip_product(0, 1), neighbours0, 2)
         acc30 = project(3, 0, 0)
-        skip1 = skip_product(1, 1)
         total0 = sb("total0", [P, N], F32)
-        skip_sum1 = sb("skip_sum1", [P, N], F32)
-        for chans in channel_pieces(NT):
-            nc.vector.tensor_tensor(skip_sum1[:, chans], skip1[:, chans], sum31[:, chans], ALU.add)
+        for chans in channel_pieces(2):
             add_weighted(total0, 3, 0, acc30, early0, chans)
 
         out_view = out.rearrange("(t p) j -> p t j", p=P)
         closing = {
             1: ((1, skip_sum3), (0, skip_sum2), (0, term[1, 2]), (1, term[1, 3])),
-            0: ((1, pair1), (1, skip_sum1), (0, total0)),
+            0: ((0, total0), (1, sum31), (1, neighbours1)),
         }
         for jp in (1, 0):
             for nt in range(NT):

@@ -238,7 +238,9 @@ def tile_list_interp_silu_kernel(
         pair0 = join("pair0", term[0, 0], term[1, 0], tag="x_bf0")
         pair1 = join("pair1", term[0, 1], term[1, 1], tag="x_bf1")
         neighbours0 = join("neighbours0", pair0, term[2, 0])
-        neighbours1 = join("neighbours1", pair1, term[2, 1])
+        high = channel_pieces(2)[1]
+        neighbours1_high = sb("neighbours1_high", [P, N // 2], F32)
+        nc.gpsimd.tensor_tensor(neighbours1_high[:], pair1[:, high], term[2, 1][:, high], ALU.add)
         sum22 = weighted_sum(2, 2, acc2[2], term[0, 2])
         sum23 = weighted_sum(2, 3, acc2[3], term[0, 3])
         sum32 = weighted_sum(3, 2, project(3, 2, 4), sum22)
@@ -255,21 +257,27 @@ def tile_list_interp_silu_kernel(
             add_weighted(total0, 3, 0, acc30, early0, chans)
 
         out_view = out.rearrange("(t p) j -> p t j", p=P)
-        closing = {
-            1: ((1, skip_sum3), (0, skip_sum2), (0, term[1, 2]), (1, term[1, 3])),
-            0: ((0, total0), (1, sum31), (1, neighbours1)),
-        }
+
+        def closing(jp, nt):
+            chans = slice(nt * P, (nt + 1) * P)
+            if jp == 1:
+                return [(1, skip_sum3[:, chans]), (0, skip_sum2[:, chans]), (0, term[1, 2][:, chans]), (1, term[1, 3][:, chans])]
+            steps = [(0, total0[:, chans]), (1, sum31[:, chans])]
+            if nt < NT // 2:
+                return steps + [(1, pair1[:, chans]), (1, term[2, 1][:, chans])]
+            return steps + [(1, neighbours1_high[:, chans.start - high.start : chans.stop - high.start])]
+
         for jp in (1, 0):
             for nt in range(NT):
                 final = psum.tile([P, 2 * P], F32, name=f"final{jp}_{nt}", tag=f"bank{FINAL_BANKS[jp][nt]}")
-                for k, (u, part) in enumerate(closing[jp]):
+                for k, (u, part) in enumerate(closing(jp, nt)):
                     nc.tensor.matmul(
                         final[:, u * P : (u + 1) * P],
-                        lhsT=part[:, nt * P : (nt + 1) * P],
+                        lhsT=part,
                         rhs=ident[:],
                         is_transpose=True,
                         start=(k == 0),
-                        stop=(k == len(closing[jp]) - 1),
+                        stop=(k == len(closing(jp, nt)) - 1),
                     )
                 result = sb(f"result{jp}_{nt}", [P, 2 * P], F32)
                 nc.scalar.activation(result[:], final[:], ACT.Silu, bias=columns[G][:, nt : nt + 1])

@@ -237,10 +237,7 @@ def tile_list_interp_silu_kernel(
 
         pair0 = join("pair0", term[0, 0], term[1, 0], tag="x_bf0")
         pair1 = join("pair1", term[0, 1], term[1, 1], tag="x_bf1")
-        neighbours0 = join("neighbours0", pair0, term[2, 0])
-        high = channel_pieces(2)[1]
-        neighbours1_high = sb("neighbours1_high", [P, N // 2], F32)
-        nc.gpsimd.tensor_tensor(neighbours1_high[:], pair1[:, high], term[2, 1][:, high], ALU.add)
+        neighbours1 = join("neighbours1", pair1, term[2, 1])
         sum22 = weighted_sum(2, 2, acc2[2], term[0, 2])
         sum23 = weighted_sum(2, 3, acc2[3], term[0, 3])
         sum32 = weighted_sum(3, 2, project(3, 2, 4), sum22)
@@ -250,7 +247,10 @@ def tile_list_interp_silu_kernel(
         skip_term1 = sb("skip_term1", [P, N], F32)
         nc.scalar.copy(skip_term1[:], skip_product(1, 2)[:])
         sum31 = weighted_sum(3, 1, project(3, 1, 3), skip_term1)
-        early0 = skip_sum(0, skip_product(0, 1), neighbours0, 2)
+        high = channel_pieces(2)[1]
+        total1_high = sb("total1_high", [P, N // 2], F32)
+        nc.gpsimd.tensor_tensor(total1_high[:], neighbours1[:, high], sum31[:, high], ALU.add)
+        early0 = skip_sum(0, skip_product(0, 1), pair0, 2)
         acc30 = project(3, 0, 0)
         total0 = sb("total0", [P, N], F32)
         for chans in channel_pieces(2):
@@ -262,10 +262,10 @@ def tile_list_interp_silu_kernel(
             chans = slice(nt * P, (nt + 1) * P)
             if jp == 1:
                 return [(1, skip_sum3[:, chans]), (0, skip_sum2[:, chans]), (0, term[1, 2][:, chans]), (1, term[1, 3][:, chans])]
-            steps = [(0, total0[:, chans]), (1, sum31[:, chans])]
+            steps = [(0, total0[:, chans]), (0, term[2, 0][:, chans])]
             if nt < NT // 2:
-                return steps + [(1, pair1[:, chans]), (1, term[2, 1][:, chans])]
-            return steps + [(1, neighbours1_high[:, chans.start - high.start : chans.stop - high.start])]
+                return steps + [(1, sum31[:, chans]), (1, neighbours1[:, chans])]
+            return steps + [(1, total1_high[:, chans.start - high.start : chans.stop - high.start])]
 
         for jp in (1, 0):
             for nt in range(NT):

from contextlib import ExitStack

import concourse.mybir as mybir
from concourse.masks import make_identity

K, L, N, T, J = 1024, 512, 512, 4096, 512
G = 4
P = 128
FLOPS = 2 * N * J * (G * K + L)

F32 = mybir.dt.float32
BF16 = mybir.dt.bfloat16
I32 = mybir.dt.int32
U32 = mybir.dt.uint32
U16 = mybir.dt.uint16
U8 = mybir.dt.uint8
FP8X4 = mybir.dt.float8_e4m3fn_x4
FP4X4 = mybir.dt.float4_e2m1fn_x4
ACT = mybir.ActivationFunctionType
ALU = mybir.AluOpType

JT = J // P
NT = N // P
LIST_COLS = J // 16
PAIR = 2 * J
FINAL_BANKS = {1: (4, 5, 6, 7), 0: (2, 3, 1, 4)}


def tile_list_interp_silu_kernel(
    tc, tab_words, tab_scales, w_words, w_scales, x, wx_words, wx_scales, iw0, iw1, iw2, iw3, b, offs, out
):
    nc = tc.nc
    with ExitStack() as ctx:
        held = ctx.enter_context(tc.tile_pool(name="held", bufs=1))
        psum = ctx.enter_context(tc.psum_pool(name="psum", bufs=1))

        def sb(name, shape, dtype, tag=None):
            return held.tile(shape, dtype, name=name, tag=tag or name, align_bytes=256)

        offsets = held.tile([P, G * LIST_COLS], U16, name="offsets")
        scale_table = sb("scale_table", [P, T // 4], I32)
        nc.sync.dma_start(scale_table[96:P, :], tab_scales.bitcast(I32).rearrange("a q t -> (a q) t"))
        nc.sync.dma_start(offsets[:], offs)
        w_planes = sb("w_planes", [P, 2, N // 4], I32)
        nc.vector.memset(w_planes[:], 0)
        rows = sb("rows", [P, P], F32)
        nc.gpsimd.memset(rows[:], 0.0)
        ident = sb("ident", [P, P], F32)
        make_identity(nc, ident[:])
        for slot, vec in enumerate((iw0, iw1, iw2)):
            nc.gpsimd.dma_start(rows[JT * slot : JT * (slot + 1), :], vec.rearrange("(t p) -> t p", p=P))
        nc.vector.memset(scale_table[0:96, :], 0)
        warm = sb("warm", [P, 16], F32)
        nc.vector.memset(warm[:, 0:1], 0.0)
        first_planes = sb("first_planes", [P, 2, PAIR // 4], I32)
        nc.vector.memset(first_planes[:], 0)
        tab_planes = [[first_planes[:, a, :] for a in range(2)]]

        w_sb = sb("w_sb", [P, 2, 2 * N], U8)
        nc.sync.dma_start(w_sb[:].bitcast(I32), w_words.bitcast(I32).rearrange("a p n -> p a n"))
        for q in (0, 2, 1, 3):
            nc.scalar.dma_start(
                w_planes[32 * q : 32 * q + 4, :, :],
                w_scales.bitcast(I32)[:, 4 * q : 4 * q + 4, :].rearrange("a r n -> r a n"),
            )
        nc.scalar.activation(warm[:, 8:9], warm[:, 0:1], ACT.Silu)
        word_table = sb("word_table", [P, T], I32)
        nc.sync.dma_start(word_table[:], tab_words[0].rearrange("p t c -> p (t c)").bitcast(I32))

        columns = {slot: sb(f"column{slot}", [P, JT], F32)[:] for slot in range(G - 1, G + 1)}

        def load_column(queue, slot, vec):
            with nc.allow_non_contiguous_dma(reason="one value a partition"):
                queue.dma_start(columns[slot], vec.rearrange("(t p) -> p t", p=P))

        turned = psum.tile([P, P], F32, name="turned", tag=f"bank{2 * JT - 2}")
        nc.tensor.matmul(turned[:], lhsT=rows[:], rhs=ident[:], is_transpose=True, start=True, stop=True)
        early = sb("early", [P, (G - 1) * JT], F32)
        nc.scalar.copy(early[:], turned[:, 0 : (G - 1) * JT])
        for slot in range(G - 1):
            columns[slot] = early[:, JT * slot : JT * (slot + 1)]

        def move_scales(h):
            picked_scales = sb(f"picked_scales{h}", [P, PAIR], U8)
            for u in range(2):
                g = 2 * h + u
                nc.vector.tensor_copy(
                    picked_scales[:, u * J : (u + 1) * J],
                    scale_table[:].bitcast(U8).indirect(offsets[:, g * LIST_COLS : (g + 1) * LIST_COLS]),
                )
            if h == 1:
                second_planes = sb("second_planes", [P, 2, PAIR // 4], I32, tag="scale_table")
                tab_planes.append([second_planes[:, a, :] for a in range(2)])
            order = [(q, a) for q in (0, 2, 1, 3) for a in (1, 0)]
            for q, a in order:
                row = 96 + 16 * a + 4 * q
                nc.sync.dma_start(tab_planes[h][a][32 * q : 32 * q + 4, :], picked_scales[row : row + 4, :].bitcast(I32))
            return picked_scales

        move_scales(0)
        x_raw = sb("x_raw", [P, 4, J], F32)
        nc.sync.dma_start(x_raw[:], x.rearrange("(p i) j -> p i j", i=4))
        late_scales = move_scales(1)
        wx_sb = sb("wx_sb", [P, 2 * N], U8)
        nc.sync.dma_start(wx_sb[:].bitcast(I32), wx_words[0].bitcast(I32))
        wx_plane = sb("wx_plane", [P, N // 4], I32, tag="picked_scales0")
        for q in range(4):
            nc.sync.dma_start(wx_plane[32 * q : 32 * q + 4, :], wx_scales.bitcast(I32)[0, 4 * q : 4 * q + 4, :])
        load_column(nc.sync, 3, iw3)
        load_column(nc.sync, 4, b)

        parted = {}
        picked = sb("picked", [P, G * J - (G - 1) * P], U32)

        def part_words(g, j0, j1):
            base = (G - 1 - g) * (J - P)
            piece = sb(f"parted{g * J + j0}", [P, 2, 2 * (j1 - j0)], U8)
            for j in range(j0, j1, P):
                parted[g * J + j] = piece[:, :, 2 * (j - j0) : 2 * (j - j0 + P)]
            nc.vector.tensor_copy(
                piece[:].bitcast(U16),
                picked[:, base + j0 : base + j1].bitcast(U16).rearrange("p (j d) -> p d j", d=2),
            )

        def gather_words(g):
            base = (G - 1 - g) * (J - P)
            nc.vector.tensor_copy(
                picked[:, base : base + J],
                word_table[:].bitcast(U32).indirect(offsets[:, g * LIST_COLS : (g + 1) * LIST_COLS]),
            )

        for g in range(2):
            gather_words(g)
            if g > 0:
                part_words(g - 1, J - P, J)
            part_words(g, 0, P)
            part_words(g, P, J - P)
        gather_words(2)
        part_words(1, J - P, J)
        for jt in (0, 2, 3):
            part_words(2, jt * P, (jt + 1) * P)
        gather_words(3)
        part_words(2, P, 2 * P)
        part_words(3, 2 * P, J)
        part_words(3, 0, 2 * P)

        warm_bank = psum.tile([P, N], F32, name="warm_bank", tag=f"bank{2 * JT - 1}")
        for r in range(3):
            nc.tensor.matmul_mx(
                out=warm_bank[:],
                lhsT=w_sb[:, 1, 0 : 2 * P].bitcast(FP4X4),
                lhsT_scale=late_scales[:, min(r, 1) * J : min(r, 1) * J + P],
                rhs=w_sb[:, 0, :].bitcast(FP4X4),
                rhs_scale=w_planes[:, 0, :].bitcast(U8),
                start=True,
                stop=True,
            )

        def project(g, jt, index):
            bank = psum.tile([P, N], F32, name=f"acc{g}_{jt}", tag=f"bank{index}")
            c0 = g * J + jt * P
            for a in range(2):
                nc.tensor.matmul_mx(
                    out=bank[:],
                    lhsT=parted[c0][:, a, :].bitcast(FP4X4),
                    lhsT_scale=tab_planes[g // 2][a][:].bitcast(U8)[:, c0 % PAIR : c0 % PAIR + P],
                    rhs=w_sb[:, a, :].bitcast(FP4X4),
                    rhs_scale=w_planes[:, a, :].bitcast(U8),
                    start=(a == 0),
                    stop=(a == 1),
                )
            return bank

        def channel_pieces(count):
            return [slice(k * N // count, (k + 1) * N // count) for k in range(count)]

        term = {}

        def scalar_term(g, jt, bank):
            term[g, jt] = sb(f"term{g}_{jt}", [P, N], F32)
            nc.scalar.activation(term[g, jt][:], bank[:], ACT.Copy, scale=columns[g][:, jt : jt + 1])

        def add_weighted(total, g, jt, bank, other, chans):
            nc.vector.scalar_tensor_tensor(
                total[:, chans], bank[:, chans], columns[g][:, jt : jt + 1], other[:, chans], ALU.mult, ALU.add
            )

        def weighted_sum(g, jt, bank, other):
            total = sb(f"sum{g}_{jt}", [P, N], F32)
            add_weighted(total, g, jt, bank, other, slice(0, N))
            return total

        def skip_sum(jt, bank, other, count):
            total = sb(f"skip_sum{jt}", [P, N], F32)
            for chans in channel_pieces(count):
                nc.vector.tensor_tensor(total[:, chans], bank[:, chans], other[:, chans], ALU.add)
            return total

        def join(name, first, second, tag=None):
            joined = sb(name, [P, N], F32, tag=tag)
            nc.gpsimd.tensor_tensor(joined[:], first[:], second[:], ALU.add)
            return joined

        for jt in range(JT):
            scalar_term(0, jt, project(0, jt, jt))

        x_codes = sb("x_codes", [P, J], U32)
        x_plane = sb("x_plane", [P, J], U8)
        for jp in range(2):
            cols = slice(2 * jp * P, 2 * (jp + 1) * P)
            x_bf = sb(f"x_bf{jp}", [P, 2 * P, 4], BF16)
            nc.scalar.copy(
                x_bf[:].rearrange("p (c j) i -> p c i j", j=4), x_raw[:, :, cols].rearrange("p i (c j) -> p c i j", j=4)
            )
            nc.vector.quantize_mx(
                out=x_codes[:, cols].bitcast(FP8X4), scales=x_plane[:, cols], in_=x_bf[:].rearrange("p j i -> p (j i)")
            )
        for jt in range(JT):
            scalar_term(1, jt, project(1, jt, JT + jt))
        acc2 = {jt: project(2, jt, jt) for jt in (2, 3, 0, 1)}
        for jt in range(2):
            scalar_term(2, jt, acc2[jt])

        def skip_product(jt, index):
            cols = slice(jt * P, (jt + 1) * P)
            bank = psum.tile([P, N], F32, name=f"skip{jt}", tag=f"bank{index}")
            nc.tensor.matmul_mx(
                out=bank[:],
                lhsT=x_codes[:, cols].bitcast(FP8X4),
                lhsT_scale=x_plane[:, cols],
                rhs=wx_sb[:].bitcast(FP4X4),
                rhs_scale=wx_plane[:].bitcast(U8),
                start=True,
                stop=True,
            )
            return bank

        pair0 = join("pair0", term[0, 0], term[1, 0], tag="x_bf0")
        pair1 = join("pair1", term[0, 1], term[1, 1], tag="x_bf1")
        neighbours1 = join("neighbours1", pair1, term[2, 1])
        sum22 = weighted_sum(2, 2, acc2[2], term[0, 2])
        sum23 = weighted_sum(2, 3, acc2[3], term[0, 3])
        sum32 = weighted_sum(3, 2, project(3, 2, 4), sum22)
        sum33 = weighted_sum(3, 3, project(3, 3, 5), sum23)
        skip_sum2 = skip_sum(2, skip_product(2, 6), sum32, 1)
        skip_sum3 = skip_sum(3, skip_product(3, 7), sum33, 1)
        skip_term1 = sb("skip_term1", [P, N], F32)
        nc.scalar.copy(skip_term1[:], skip_product(1, 2)[:])
        sum31 = weighted_sum(3, 1, project(3, 1, 3), skip_term1)
        high = channel_pieces(2)[1]
        total1_high = sb("total1_high", [P, N // 2], F32)
        nc.gpsimd.tensor_tensor(total1_high[:], neighbours1[:, high], sum31[:, high], ALU.add)
        early0 = skip_sum(0, skip_product(0, 1), pair0, 2)
        acc30 = project(3, 0, 0)
        total0 = sb("total0", [P, N], F32)
        for chans in channel_pieces(2):
            add_weighted(total0, 3, 0, acc30, early0, chans)

        out_view = out.rearrange("(t p) j -> p t j", p=P)

        def closing(jp, nt):
            chans = slice(nt * P, (nt + 1) * P)
            if jp == 1:
                return [(1, skip_sum3[:, chans]), (0, skip_sum2[:, chans]), (0, term[1, 2][:, chans]), (1, term[1, 3][:, chans])]
            steps = [(0, total0[:, chans]), (0, term[2, 0][:, chans])]
            if nt < NT // 2:
                return steps + [(1, sum31[:, chans]), (1, neighbours1[:, chans])]
            return steps + [(1, total1_high[:, chans.start - high.start : chans.stop - high.start])]

        for jp in (1, 0):
            for nt in range(NT):
                final = psum.tile([P, 2 * P], F32, name=f"final{jp}_{nt}", tag=f"bank{FINAL_BANKS[jp][nt]}")
                for k, (u, part) in enumerate(closing(jp, nt)):
                    nc.tensor.matmul(
                        final[:, u * P : (u + 1) * P],
                        lhsT=part,
                        rhs=ident[:],
                        is_transpose=True,
                        start=(k == 0),
                        stop=(k == len(closing(jp, nt)) - 1),
                    )
                result = sb(f"result{jp}_{nt}", [P, 2 * P], F32)
                nc.scalar.activation(result[:], final[:], ACT.Silu, bias=columns[G][:, nt : nt + 1])
                nc.sync.dma_start(out_view[:, nt, 2 * jp * P : 2 * (jp + 1) * P], result[:])
